import numpy as np
import ml_dtypes


def mxq(x, axis, fmt="e4m3"):
    dtype, down = {"e4m3": (ml_dtypes.float8_e4m3fn, 7), "e5m2": (ml_dtypes.float8_e5m2, 14)}[fmt]
    v = np.moveaxis(np.asarray(x, np.float32).astype(ml_dtypes.bfloat16).astype(np.float64), axis, -1)
    blocks = v.reshape(v.shape[:-1] + (-1, 32))
    amax = np.abs(blocks).max(-1, keepdims=True)
    byte = np.maximum(np.where(amax > 0, np.frexp(amax)[1] - 1 + 127, 0) - down, 1)
    scale = np.exp2(byte - 127.0)
    codes = (blocks / scale).astype(np.float32).astype(dtype).astype(np.float64)
    return np.moveaxis((codes * scale).reshape(v.shape), -1, axis)


WIDE = False


def mx_kscale(k):
    if not WIDE:
        return np.ones(k)
    levels = np.array([10, -10, 5, -5, 0])
    if k % 512:
        return np.exp2(np.random.permutation(np.resize(levels, k // 32))).repeat(32)
    a = np.empty((k // 512, 16))
    for p in range(k // 512):
        a[p, :8] = np.random.permutation(np.resize(levels, 8))
        for g in range(8):
            far = levels[np.abs(levels - a[p, g]) >= 10]
            a[p, g + 8] = far[np.random.randint(len(far))]
    return np.exp2(a.ravel()).repeat(32)


def f64(x):
    return np.asarray(x).astype(np.float64)


def striped(idx):
    return np.tile(np.asarray(idx).reshape(-1, 16).T, (8, 1)).astype(np.uint16)


def unstriped(offs):
    return offs[:16].T.reshape(-1).astype(np.int64)


E2M1 = np.array([0.0, 0.5, 1.0, 1.5, 2.0, 3.0, 4.0, 6.0, -0.0, -0.5, -1.0, -1.5, -2.0, -3.0, -4.0, -6.0])


def pack_weight(w, fmt):
    k, n = w.shape
    w = f64(np.asarray(w, np.float32).astype(ml_dtypes.bfloat16)).reshape(k // 32, 32, n)
    amax = np.abs(w).max(1)
    if fmt == "e4m3":
        byte = np.frexp(amax)[1] - 1 + 127 - 7
    else:
        mant, ex = np.frexp(amax / 6.0)
        byte = np.where(mant > 0.5, ex, ex - 1) + 127
    byte = np.clip(np.where(amax > 0, byte, 1), 1, 254)
    scaled = (w * np.exp2(127.0 - byte)[:, None, :]).reshape(k, n).astype(np.float32)
    by_word = np.ascontiguousarray(scaled.reshape(k // 512, 128, 4, n).transpose(0, 1, 3, 2))
    if fmt == "e4m3":
        words = by_word.astype(ml_dtypes.float8_e4m3fn).view(np.uint8)
    else:
        c = by_word.astype(ml_dtypes.float4_e2m1fn).view(np.uint8) & 0xF
        words = (c[..., 0::2] | (c[..., 1::2] << 4)).reshape(k // 512, 128, 2 * n)
    return np.ascontiguousarray(words), np.ascontiguousarray(byte.astype(np.uint8).reshape(k // 512, 16, n))


def unpack_weight(words, scales, fmt):
    g, _, n = scales.shape
    words = np.ascontiguousarray(words).reshape(g, 128, n, -1)
    if fmt == "e4m3":
        vals = words.view(ml_dtypes.float8_e4m3fn).astype(np.float64)
    else:
        nib = np.empty((g, 128, n, 4), np.uint8)
        nib[..., 0::2] = words & 0xF
        nib[..., 1::2] = words >> 4
        vals = E2M1[nib]
    vals = vals * np.repeat(np.exp2(scales.astype(np.float64) - 127.0), 8, axis=1)[..., None]
    return vals.transpose(0, 1, 3, 2).reshape(g * 512, n)


B, N, T, D, DV, NQ = 1, 512, 2048, 512, 128, 128


def setup_inputs():
    n = np.random.standard_normal
    idx = np.sort(np.random.permutation(T)[:B * N].reshape(B, N), axis=1).reshape(-1)
    s = mx_kscale(D)[:, None]
    u = np.ones(T)
    u[idx] = mx_kscale(B * N)
    r = np.random.uniform(0.5, 2.0, T)
    qp = [pack_weight(x, "e4m3") for x in n((B, D, NQ)) * s * (0.80 / np.sqrt(D))]
    k = n((D, T)) / s
    v = n((DV, T)) / (u * r)
    kp = pack_weight(k, "e4m3")
    return {
        "q_words": np.stack([x[0] for x in qp]),
        "q_scales": np.stack([x[1] for x in qp]),
        "k_words": kp[0],
        "k_scales": kp[1],
        "vT": v.astype(np.float32),
        "vs": np.tile(u * r, (128, 1)).astype(np.float32),
        "sink": (2.0 + 3.0 * n((B, NQ, 1))).astype(np.float32),
        "og": n((B, NQ, DV)).astype(np.float32),
        "offs": striped(idx),
    }


def reference(q_words, q_scales, k_words, k_scales, vT, vs, sink, og, offs):
    idx = unstriped(offs)
    k = unpack_weight(k_words, k_scales, "e4m3")
    v = f64(vT)
    pick = lambda x: x[:, idx].reshape(x.shape[0], B, N).transpose(1, 0, 2)
    q = np.stack([unpack_weight(q_words[b], q_scales[b], "e4m3") for b in range(B)])
    score = q.transpose(0, 2, 1) @ pick(k)
    m = np.maximum(score.max(-1, keepdims=True), f64(sink))
    p = np.exp(score - m)
    total = p.sum(-1, keepdims=True) + np.exp(f64(sink) - m)
    w = p * pick(f64(vs))[:, :1, :]
    y = mxq(w, 2, "e4m3") @ mxq(pick(v).transpose(0, 2, 1), 1, "e4m3")
    y = y / total
    y = y / (1.0 + np.exp(-f64(og)))
    return y

@@ -1,0 +1,191 @@
+from contextlib import ExitStack
+
+import concourse.mybir as mybir
+
+P = 128
+T = 2048
+N = 512
+NQ = 128
+DV = 128
+D = 512
+PACK = 4
+HALF = N // 2
+VS_ROW = 16
+
+FLOPS = 2 * NQ * N * D + 2 * NQ * N * DV
+BYTES = P * T * 4 + 16 * T + P * NQ * 4 + 16 * NQ + DV * T * 4 + T * 4 + NQ * 4 + 2 * NQ * DV * 4 + P * (N // 16) * 2
+
+F32 = mybir.dt.float32
+BF16 = mybir.dt.bfloat16
+I32 = mybir.dt.int32
+U32 = mybir.dt.uint32
+U16 = mybir.dt.uint16
+U8 = mybir.dt.uint8
+FP8X4 = mybir.dt.float8_e4m3fn_x4
+ALU = mybir.AluOpType
+ACT = mybir.ActivationFunctionType
+
+
+def tile_attend_soft_sink_gate_srtq128n512t2048_kernel(
+    tc, q_words, q_scales, k_words, k_scales, vT, vs, sink, og, offs, out
+):
+    nc = tc.nc
+    with ExitStack() as ctx:
+        sb = ctx.enter_context(tc.tile_pool(name="sb", bufs=1))
+        ps = ctx.enter_context(tc.psum_pool(name="ps", bufs=1))
+
+        offsets = sb.tile([P, N // 16], U16, name="offsets")
+        kw_pool = sb.tile([P, T], U32, name="kw_pool", align_bytes=64)
+        ks_pool = sb.tile([P, T], U8, name="ks_pool", tag="slot_a", align_bytes=64)
+        v_pool = sb.tile([P, T], F32, name="v_pool", align_bytes=64)
+        vs_pool = sb.tile([P, T], F32, name="vs_pool", tag="slot_b", align_bytes=64)
+        qw = sb.tile([P, NQ], U32, name="qw", align_bytes=64)
+        qs = sb.tile([P, NQ], U8, name="qs", align_bytes=64)
+        sink_col = sb.tile([P, 1], F32, name="sink_col")
+        gate_in = sb.tile([P, DV], F32, name="gate_in")
+        ident = sb.tile([P, P], F32, name="ident", align_bytes=64)
+
+        nc.vector.memset(ks_pool[:].bitcast(I32), 0)
+        nc.vector.memset(qs[:].bitcast(I32), 0)
+        nc.vector.memset(vs_pool[:].bitcast(I32), 0)
+        q_rows = q_scales[0, 0].bitcast(I32)
+
+        nc.sync.dma_start(offsets[:], offs)
+        nc.sync.dma_start(kw_pool[:].bitcast(I32), k_words[0].rearrange("p n t -> p (n t)").bitcast(I32))
+        nc.scalar.dma_start(qw[:].bitcast(I32), q_words[0, 0].rearrange("p n t -> p (n t)").bitcast(I32))
+        for quad in range(4):
+            nc.scalar.dma_start(
+                ks_pool[32 * quad : 32 * quad + 4, :].bitcast(I32), k_scales[0, 4 * quad : 4 * quad + 4, :].bitcast(I32)
+            )
+        nc.scalar.dma_start(qs[96:100, :].bitcast(I32), q_rows[12:16, :])
+        nc.gpsimd.dma_start(qs[0:70, :].bitcast(I32), q_rows[0:14, :].unsqueeze(0).broadcast_to([5, 14, NQ // 4]))
+        nc.scalar.dma_start(vs_pool[VS_ROW : VS_ROW + 1, :], vs[0:1, :])
+        nc.sync.dma_start(v_pool[:], vT)
+        nc.gpsimd.dma_start(sink_col[:], sink[0])
+        ones = sb.tile([P, 32], F32, name="ones", align_bytes=64)
+        own_quad = sb.tile([P, 4], F32, name="own_quad")
+        nc.gpsimd.memset(ones[:], 1.0)
+        nc.gpsimd.memset(own_quad[:], 0.0)
+        for quad in range(4):
+            nc.gpsimd.memset(own_quad[32 * quad : 32 * quad + 32, quad : quad + 1], 1.0)
+        ramp = sb.tile([P, 32], F32, name="ramp", align_bytes=64)
+        ramp_t = sb.tile([P, 32], F32, name="ramp_t", align_bytes=64)
+        nc.vector.tensor_tensor_scan(ramp[:], ones[:], ones[:], 0.0, ALU.mult, ALU.add)
+        nc.vector.transpose(ramp_t[:], ramp[:])
+        nc.vector.scalar_tensor_tensor(
+            ident[:].rearrange("p (b j) -> p b j", j=32),
+            ramp[:].unsqueeze(1).broadcast_to([P, 4, 32]),
+            ramp_t[:, 0:1],
+            own_quad[:].unsqueeze(2).broadcast_to([P, 4, 32]),
+            ALU.is_equal,
+            ALU.mult,
+        )
+        nc.gpsimd.dma_start(gate_in[:], og[0])
+
+        ks_g = sb.tile([P, N], U8, name="ks_g", align_bytes=64)
+        nc.vector.tensor_copy(ks_g[:], ks_pool[:].indirect(offsets[:]))
+        vs_g = sb.tile([P, N], F32, name="vs_g", align_bytes=64)
+        nc.vector.tensor_copy(vs_g[:], vs_pool[:].indirect(offsets[:]))
+
+        neg = sb.tile([P, N + 1], F32, name="neg", tag="slot_c", align_bytes=64)
+        nc.scalar.mul(neg[:, N : N + 1], sink_col[:], -1.0)
+        vs_d = sb.tile([P, PACK, P], F32, name="vs_d", align_bytes=64)
+        nc.scalar.copy(vs_d[:], vs_g[:].rearrange("p (s t) -> p t s", t=PACK))
+
+        kw_g = [sb.tile([P, HALF], U32, name=f"kw_g{h}", tag=("slot_a", "slot_b")[h], align_bytes=64) for h in range(2)]
+        scores = [ps.tile([P, HALF], F32, name=f"scores{h}", tag=f"bank{h}") for h in range(2)]
+        for h in range(2):
+            cols = HALF // 16
+            nc.vector.tensor_copy(kw_g[h][:], kw_pool[:].indirect(offsets[:, h * cols : (h + 1) * cols]))
+            nc.tensor.matmul_mx(
+                out=scores[h][:],
+                lhsT=qw[:].bitcast(FP8X4),
+                lhsT_scale=qs[:],
+                rhs=kw_g[h][:].bitcast(FP8X4),
+                rhs_scale=ks_g[:, h * HALF : (h + 1) * HALF],
+                start=True,
+                stop=True,
+            )
+
+        neg_dealt = neg[:, 0:N].rearrange("q (t s) -> q t s", t=PACK)
+        neg_max = [sb.tile([P, 1], F32, name=f"neg_max{h}") for h in range(2)]
+        start_value = neg[:, N : N + 1]
+        for h in range(2):
+            nc.vector.tensor_scalar(
+                neg_dealt[:, :, h * 64 : (h + 1) * 64],
+                scores[h][:].rearrange("q (s t) -> q t s", t=PACK),
+                -1.0,
+                start_value,
+                ALU.mult,
+                ALU.min,
+                accum_out=neg_max[h][:],
+            )
+            start_value = neg_max[h][:]
+
+        vs_ps = ps.tile([P, PACK, P], F32, name="vs_ps", tag="bank0")
+        for t in range(PACK):
+            nc.tensor.transpose(vs_ps[:, t, :], vs_d[:, t, :], ident[:])
+
+        p_sb = sb.tile([P, N + 1], F32, name="p_sb", align_bytes=64)
+        sums = [sb.tile([P, 1], F32, name=f"sums{h}") for h in range(2)]
+        p_ps = ps.tile([P, PACK, P], F32, name="p_ps")
+        for h in range(2):
+            cols = slice(h * HALF, (h + 1) * HALF + h)
+            nc.scalar.activation(p_sb[:, cols], neg[:, cols], ACT.Exp, bias=neg_max[1][:], scale=-1.0, accum_out=sums[h][:])
+            for t in (2 * h, 2 * h + 1):
+                nc.tensor.transpose(p_ps[:, t, :], p_sb[:, t * P : (t + 1) * P], ident[:])
+
+        vs_col = sb.tile([P, PACK], F32, name="vs_col", tag="slot_c", align_bytes=64)
+        nc.scalar.copy(vs_col[:], vs_ps[:, :, VS_ROW])
+
+        v_g = sb.tile([P, N], BF16, name="v_g", tag="slot_b", align_bytes=64)
+        nc.vector.tensor_copy(v_g[:], v_pool[:].indirect(offsets[:]))
+        v_ps = ps.tile([P, 2, DV], F32, name="v_ps")
+        v_words = v_g[:].bitcast(F32)
+        for u in range(2):
+            nc.tensor.transpose(v_ps[:, u, :], v_words[:, u::2], ident[:])
+        v_q = sb.tile([P, DV, PACK], BF16, name="v_q", align_bytes=64)
+        nc.scalar.copy(v_q[:].bitcast(F32), v_ps[:].rearrange("s u e -> s e u"))
+
+        w_q = sb.tile([P, NQ, PACK], BF16, name="w_q", align_bytes=64)
+        nc.vector.tensor_tensor(
+            w_q[:],
+            p_ps[:].rearrange("s t q -> s q t"),
+            vs_col[:].unsqueeze(1).broadcast_to([P, NQ, PACK]),
+            ALU.mult,
+        )
+
+        total = sb.tile([P, 1], F32, name="total")
+        nc.scalar.activation(total[:], sums[0][:], ACT.Identity, bias=sums[1][:])
+        inv_total = sb.tile([P, 1], F32, name="inv_total")
+        nc.vector.reciprocal(inv_total[:], total[:])
+
+        w_codes = sb.tile([P, NQ], U32, name="w_codes", align_bytes=64)
+        w_scales = sb.tile([P, NQ], U8, name="w_scales", align_bytes=64)
+        nc.vector.quantize_mx(
+            out=w_codes[:].bitcast(FP8X4), scales=w_scales[:], in_=w_q[:].rearrange("s q t -> s (q t)")
+        )
+        v_codes = sb.tile([P, DV], U32, name="v_codes", align_bytes=64)
+        v_scales = sb.tile([P, DV], U8, name="v_scales", align_bytes=64)
+        nc.vector.quantize_mx(
+            out=v_codes[:].bitcast(FP8X4), scales=v_scales[:], in_=v_q[:].rearrange("s e t -> s (e t)")
+        )
+
+        half_tanh = sb.tile([P, DV], F32, name="half_tanh")
+        nc.scalar.activation(half_tanh[:], gate_in[:], ACT.Tanh, scale=0.5)
+        gate = sb.tile([P, DV], F32, name="gate")
+        nc.scalar.activation(gate[:], half_tanh[:], ACT.Copy, bias=0.5, scale=0.5)
+
+        y_ps = ps.tile([P, DV], F32, name="y_ps")
+        nc.tensor.matmul_mx(
+            out=y_ps[:],
+            lhsT=w_codes[:].bitcast(FP8X4),
+            lhsT_scale=w_scales[:],
+            rhs=v_codes[:].bitcast(FP8X4),
+            rhs_scale=v_scales[:],
+            start=True,
+            stop=True,
+        )
+        y = sb.tile([P, DV], F32, name="y")
+        nc.vector.scalar_tensor_tensor(y[:], y_ps[:], inv_total[:], gate[:], ALU.mult, ALU.mult)
+        nc.sync.dma_start(out[0], y[:])

@@ -11,6 +11,7 @@ D = 512
 PACK = 4
 HALF = N // 2
 VS_ROW = 16
+K_CUT = (512, 1408)
 
 FLOPS = 2 * NQ * N * D + 2 * NQ * N * DV
 BYTES = P * T * 4 + 16 * T + P * NQ * 4 + 16 * NQ + DV * T * 4 + T * 4 + NQ * 4 + 2 * NQ * DV * 4 + P * (N // 16) * 2
@@ -46,28 +47,34 @@ def tile_attend_soft_sink_gate_srtq128n512t2048_kernel(
         ident = sb.tile([P, P], F32, name="ident", align_bytes=64)
 
         nc.vector.memset(ks_pool[:].bitcast(I32), 0)
-        nc.vector.memset(qs[:].bitcast(I32), 0)
         nc.vector.memset(vs_pool[:].bitcast(I32), 0)
+        nc.vector.memset(qs[:].bitcast(I32), 0)
         q_rows = q_scales[0, 0].bitcast(I32)
+        k_rows = k_scales[0].bitcast(I32)
+        k_all = k_words[0].rearrange("p n t -> p (n t)").bitcast(I32)
+
+        def load_keys(first, last):
+            nc.sync.dma_start(kw_pool[:, first:last].bitcast(I32), k_all[:, first:last])
 
         nc.sync.dma_start(offsets[:], offs)
-        nc.sync.dma_start(kw_pool[:].bitcast(I32), k_words[0].rearrange("p n t -> p (n t)").bitcast(I32))
         nc.scalar.dma_start(qw[:].bitcast(I32), q_words[0, 0].rearrange("p n t -> p (n t)").bitcast(I32))
+        load_keys(0, K_CUT[0])
         for quad in range(4):
-            nc.scalar.dma_start(
-                ks_pool[32 * quad : 32 * quad + 4, :].bitcast(I32), k_scales[0, 4 * quad : 4 * quad + 4, :].bitcast(I32)
-            )
-        nc.scalar.dma_start(qs[96:100, :].bitcast(I32), q_rows[12:16, :])
-        nc.gpsimd.dma_start(qs[0:70, :].bitcast(I32), q_rows[0:14, :].unsqueeze(0).broadcast_to([5, 14, NQ // 4]))
-        nc.scalar.dma_start(vs_pool[VS_ROW : VS_ROW + 1, :], vs[0:1, :])
+            queue = nc.sync if quad < 2 else nc.scalar
+            queue.dma_start(ks_pool[32 * quad : 32 * quad + 4, :].bitcast(I32), k_rows[4 * quad : 4 * quad + 4, :])
+        load_keys(K_CUT[0], K_CUT[1])
+        nc.sync.dma_start(vs_pool[VS_ROW : VS_ROW + 1, :], vs[0:1, :])
+        load_keys(K_CUT[1], T)
+        for quad in range(4):
+            nc.sync.dma_start(qs[32 * quad : 32 * quad + 4, :].bitcast(I32), q_rows[4 * quad : 4 * quad + 4, :])
         nc.sync.dma_start(v_pool[:], vT)
-        nc.gpsimd.dma_start(sink_col[:], sink[0])
         ones = sb.tile([P, 32], F32, name="ones", align_bytes=64)
         own_quad = sb.tile([P, 4], F32, name="own_quad")
         nc.gpsimd.memset(ones[:], 1.0)
         nc.gpsimd.memset(own_quad[:], 0.0)
         for quad in range(4):
             nc.gpsimd.memset(own_quad[32 * quad : 32 * quad + 32, quad : quad + 1], 1.0)
+        nc.gpsimd.dma_start(sink_col[:], sink[0])
         ramp = sb.tile([P, 32], F32, name="ramp", align_bytes=64)
         ramp_t = sb.tile([P, 32], F32, name="ramp_t", align_bytes=64)
         nc.vector.tensor_tensor_scan(ramp[:], ones[:], ones[:], 0.0, ALU.mult, ALU.add)

@@ -42,13 +42,25 @@ def tile_attend_soft_sink_gate_srtq128n512t2048_kernel(
         vs_pool = sb.tile([P, T], F32, name="vs_pool", tag="slot_b", align_bytes=64)
         qw = sb.tile([P, NQ], U32, name="qw", align_bytes=64)
         qs = sb.tile([P, NQ], U8, name="qs", align_bytes=64)
-        sink_col = sb.tile([P, 1], F32, name="sink_col")
         gate_in = sb.tile([P, DV], F32, name="gate_in")
         ident = sb.tile([P, P], F32, name="ident", align_bytes=64)
 
+        ones = sb.tile([P, 32], F32, name="ones", align_bytes=64)
+        ramp = sb.tile([P, 32], F32, name="ramp", align_bytes=64)
+        ramp_t = sb.tile([P, 32], F32, name="ramp_t", align_bytes=64)
+        distance = sb.tile([P, 32], F32, name="distance", align_bytes=64)
+
         nc.vector.memset(ks_pool[:].bitcast(I32), 0)
+        nc.vector.memset(ones[:], 1.0)
         nc.vector.memset(vs_pool[:].bitcast(I32), 0)
+        nc.vector.tensor_tensor_scan(ramp[:], ones[:], ones[:], 0.0, ALU.mult, ALU.add)
         nc.vector.memset(qs[:].bitcast(I32), 0)
+        nc.vector.memset(ident[:], 0.0)
+        nc.vector.transpose(ramp_t[:], ramp[:])
+        nc.scalar.activation(distance[:], ramp[:], ACT.Abs, bias=ramp_t[:, 0:1], scale=-1.0)
+        for quad in range(4):
+            rows = slice(32 * quad, 32 * quad + 32)
+            nc.scalar.activation(ident[rows, rows], distance[rows, :], ACT.Relu, bias=ramp[rows, 0:1], scale=-1.0)
         q_rows = q_scales[0, 0].bitcast(I32)
         k_rows = k_scales[0].bitcast(I32)
         k_all = k_words[0].rearrange("p n t -> p (n t)").bitcast(I32)
@@ -68,26 +80,9 @@ def tile_attend_soft_sink_gate_srtq128n512t2048_kernel(
         for quad in range(4):
             nc.sync.dma_start(qs[32 * quad : 32 * quad + 4, :].bitcast(I32), q_rows[4 * quad : 4 * quad + 4, :])
         nc.sync.dma_start(v_pool[:], vT)
-        ones = sb.tile([P, 32], F32, name="ones", align_bytes=64)
-        own_quad = sb.tile([P, 4], F32, name="own_quad")
-        nc.gpsimd.memset(ones[:], 1.0)
-        nc.gpsimd.memset(own_quad[:], 0.0)
-        for quad in range(4):
-            nc.gpsimd.memset(own_quad[32 * quad : 32 * quad + 32, quad : quad + 1], 1.0)
+        sink_col = sb.tile([P, 1], F32, name="sink_col")
         nc.gpsimd.dma_start(sink_col[:], sink[0])
-        ramp = sb.tile([P, 32], F32, name="ramp", align_bytes=64)
-        ramp_t = sb.tile([P, 32], F32, name="ramp_t", align_bytes=64)
-        nc.vector.tensor_tensor_scan(ramp[:], ones[:], ones[:], 0.0, ALU.mult, ALU.add)
-        nc.vector.transpose(ramp_t[:], ramp[:])
-        nc.vector.scalar_tensor_tensor(
-            ident[:].rearrange("p (b j) -> p b j", j=32),
-            ramp[:].unsqueeze(1).broadcast_to([P, 4, 32]),
-            ramp_t[:, 0:1],
-            own_quad[:].unsqueeze(2).broadcast_to([P, 4, 32]),
-            ALU.is_equal,
-            ALU.mult,
-        )
-        nc.gpsimd.dma_start(gate_in[:], og[0])
+        nc.sync.dma_start(gate_in[:], og[0])
 
         ks_g = sb.tile([P, N], U8, name="ks_g", align_bytes=64)
         nc.vector.tensor_copy(ks_g[:], ks_pool[:].indirect(offsets[:]))
@@ -115,7 +110,7 @@ def tile_attend_soft_sink_gate_srtq128n512t2048_kernel(
             )
 
         neg_dealt = neg[:, 0:N].rearrange("q (t s) -> q t s", t=PACK)
-        neg_max = [sb.tile([P, 1], F32, name=f"neg_max{h}") for h in range(2)]
+        neg_max = [sb.tile([P, 1], F32, name=f"neg_max{h}", tag=f"slot_m{h}") for h in range(2)]
         start_value = neg[:, N : N + 1]
         for h in range(2):
             nc.vector.tensor_scalar(
@@ -154,6 +149,11 @@ def tile_attend_soft_sink_gate_srtq128n512t2048_kernel(
         v_q = sb.tile([P, DV, PACK], BF16, name="v_q", align_bytes=64)
         nc.scalar.copy(v_q[:].bitcast(F32), v_ps[:].rearrange("s u e -> s e u"))
 
+        total = sb.tile([P, 1], F32, name="total")
+        nc.scalar.activation(total[:], sums[0][:], ACT.Identity, bias=sums[1][:])
+        inv_total = sb.tile([P, 1], F32, name="inv_total")
+        nc.vector.reciprocal(inv_total[:], total[:])
+
         w_q = sb.tile([P, NQ, PACK], BF16, name="w_q", align_bytes=64)
         nc.vector.tensor_tensor(
             w_q[:],
@@ -162,23 +162,18 @@ def tile_attend_soft_sink_gate_srtq128n512t2048_kernel(
             ALU.mult,
         )
 
-        total = sb.tile([P, 1], F32, name="total")
-        nc.scalar.activation(total[:], sums[0][:], ACT.Identity, bias=sums[1][:])
-        inv_total = sb.tile([P, 1], F32, name="inv_total")
-        nc.vector.reciprocal(inv_total[:], total[:])
-
-        w_codes = sb.tile([P, NQ], U32, name="w_codes", align_bytes=64)
-        w_scales = sb.tile([P, NQ], U8, name="w_scales", align_bytes=64)
-        nc.vector.quantize_mx(
-            out=w_codes[:].bitcast(FP8X4), scales=w_scales[:], in_=w_q[:].rearrange("s q t -> s (q t)")
-        )
         v_codes = sb.tile([P, DV], U32, name="v_codes", align_bytes=64)
         v_scales = sb.tile([P, DV], U8, name="v_scales", align_bytes=64)
         nc.vector.quantize_mx(
             out=v_codes[:].bitcast(FP8X4), scales=v_scales[:], in_=v_q[:].rearrange("s e t -> s (e t)")
         )
+        w_codes = sb.tile([P, NQ], U32, name="w_codes", align_bytes=64)
+        w_scales = sb.tile([P, NQ], U8, name="w_scales", align_bytes=64)
+        nc.vector.quantize_mx(
+            out=w_codes[:].bitcast(FP8X4), scales=w_scales[:], in_=w_q[:].rearrange("s q t -> s (q t)")
+        )
 
-        half_tanh = sb.tile([P, DV], F32, name="half_tanh")
+        half_tanh = sb.tile([P, DV], F32, name="half_tanh", tag="slot_m1")
         nc.scalar.activation(half_tanh[:], gate_in[:], ACT.Tanh, scale=0.5)
         gate = sb.tile([P, DV], F32, name="gate")
         nc.scalar.activation(gate[:], half_tanh[:], ACT.Copy, bias=0.5, scale=0.5)

@@ -82,7 +82,7 @@ def tile_attend_soft_sink_gate_srtq128n512t2048_kernel(
         nc.sync.dma_start(v_pool[:], vT)
         sink_col = sb.tile([P, 1], F32, name="sink_col")
         nc.gpsimd.dma_start(sink_col[:], sink[0])
-        nc.sync.dma_start(gate_in[:], og[0])
+        nc.gpsimd.dma_start(gate_in[:], og[0])
 
         ks_g = sb.tile([P, N], U8, name="ks_g", align_bytes=64)
         nc.vector.tensor_copy(ks_g[:], ks_pool[:].indirect(offsets[:]))
@@ -110,7 +110,7 @@ def tile_attend_soft_sink_gate_srtq128n512t2048_kernel(
             )
 
         neg_dealt = neg[:, 0:N].rearrange("q (t s) -> q t s", t=PACK)
-        neg_max = [sb.tile([P, 1], F32, name=f"neg_max{h}", tag=f"slot_m{h}") for h in range(2)]
+        neg_max = [sb.tile([P, 1], F32, name=f"neg_max{h}") for h in range(2)]
         start_value = neg[:, N : N + 1]
         for h in range(2):
             nc.vector.tensor_scalar(
@@ -162,18 +162,18 @@ def tile_attend_soft_sink_gate_srtq128n512t2048_kernel(
             ALU.mult,
         )
 
-        v_codes = sb.tile([P, DV], U32, name="v_codes", align_bytes=64)
-        v_scales = sb.tile([P, DV], U8, name="v_scales", align_bytes=64)
-        nc.vector.quantize_mx(
-            out=v_codes[:].bitcast(FP8X4), scales=v_scales[:], in_=v_q[:].rearrange("s e t -> s (e t)")
-        )
         w_codes = sb.tile([P, NQ], U32, name="w_codes", align_bytes=64)
         w_scales = sb.tile([P, NQ], U8, name="w_scales", align_bytes=64)
         nc.vector.quantize_mx(
             out=w_codes[:].bitcast(FP8X4), scales=w_scales[:], in_=w_q[:].rearrange("s q t -> s (q t)")
         )
+        v_codes = sb.tile([P, DV], U32, name="v_codes", align_bytes=64)
+        v_scales = sb.tile([P, DV], U8, name="v_scales", align_bytes=64)
+        nc.vector.quantize_mx(
+            out=v_codes[:].bitcast(FP8X4), scales=v_scales[:], in_=v_q[:].rearrange("s e t -> s (e t)")
+        )
 
-        half_tanh = sb.tile([P, DV], F32, name="half_tanh", tag="slot_m1")
+        half_tanh = sb.tile([P, DV], F32, name="half_tanh", tag="slot_b", align_bytes=64)
         nc.scalar.activation(half_tanh[:], gate_in[:], ACT.Tanh, scale=0.5)
         gate = sb.tile([P, DV], F32, name="gate")
         nc.scalar.activation(gate[:], half_tanh[:], ACT.Copy, bias=0.5, scale=0.5)

@@ -10,8 +10,8 @@ DV = 128
 D = 512
 PACK = 4
 HALF = N // 2
-VS_ROW = 16
-K_CUT = (512, 1408)
+VS_ROW = P - 1
+K_CUT = 640
 
 FLOPS = 2 * NQ * N * D + 2 * NQ * N * DV
 BYTES = P * T * 4 + 16 * T + P * NQ * 4 + 16 * NQ + DV * T * 4 + T * 4 + NQ * 4 + 2 * NQ * DV * 4 + P * (N // 16) * 2
@@ -51,16 +51,8 @@ def tile_attend_soft_sink_gate_srtq128n512t2048_kernel(
         distance = sb.tile([P, 32], F32, name="distance", align_bytes=64)
 
         nc.vector.memset(ks_pool[:].bitcast(I32), 0)
-        nc.vector.memset(ones[:], 1.0)
-        nc.vector.memset(vs_pool[:].bitcast(I32), 0)
-        nc.vector.tensor_tensor_scan(ramp[:], ones[:], ones[:], 0.0, ALU.mult, ALU.add)
         nc.vector.memset(qs[:].bitcast(I32), 0)
-        nc.vector.memset(ident[:], 0.0)
-        nc.vector.transpose(ramp_t[:], ramp[:])
-        nc.scalar.activation(distance[:], ramp[:], ACT.Abs, bias=ramp_t[:, 0:1], scale=-1.0)
-        for quad in range(4):
-            rows = slice(32 * quad, 32 * quad + 32)
-            nc.scalar.activation(ident[rows, rows], distance[rows, :], ACT.Relu, bias=ramp[rows, 0:1], scale=-1.0)
+        nc.vector.memset(vs_pool[0:VS_ROW, :].bitcast(I32), 0)
         q_rows = q_scales[0, 0].bitcast(I32)
         k_rows = k_scales[0].bitcast(I32)
         k_all = k_words[0].rearrange("p n t -> p (n t)").bitcast(I32)
@@ -68,26 +60,34 @@ def tile_attend_soft_sink_gate_srtq128n512t2048_kernel(
         def load_keys(first, last):
             nc.sync.dma_start(kw_pool[:, first:last].bitcast(I32), k_all[:, first:last])
 
+        sink_col = sb.tile([P, 1], F32, name="sink_col")
         nc.sync.dma_start(offsets[:], offs)
-        nc.scalar.dma_start(qw[:].bitcast(I32), q_words[0, 0].rearrange("p n t -> p (n t)").bitcast(I32))
-        load_keys(0, K_CUT[0])
+        nc.scalar.dma_start(vs_pool[VS_ROW : VS_ROW + 1, :], vs[0:1, :])
+        load_keys(0, K_CUT)
         for quad in range(4):
-            queue = nc.sync if quad < 2 else nc.scalar
+            queue = nc.sync if quad < 3 else nc.scalar
             queue.dma_start(ks_pool[32 * quad : 32 * quad + 4, :].bitcast(I32), k_rows[4 * quad : 4 * quad + 4, :])
-        load_keys(K_CUT[0], K_CUT[1])
-        nc.sync.dma_start(vs_pool[VS_ROW : VS_ROW + 1, :], vs[0:1, :])
-        load_keys(K_CUT[1], T)
+        load_keys(K_CUT, T)
+        nc.sync.dma_start(qw[:].bitcast(I32), q_words[0, 0].rearrange("p n t -> p (n t)").bitcast(I32))
         for quad in range(4):
             nc.sync.dma_start(qs[32 * quad : 32 * quad + 4, :].bitcast(I32), q_rows[4 * quad : 4 * quad + 4, :])
+        nc.sync.dma_start(sink_col[:], sink[0])
         nc.sync.dma_start(v_pool[:], vT)
-        sink_col = sb.tile([P, 1], F32, name="sink_col")
-        nc.gpsimd.dma_start(sink_col[:], sink[0])
-        nc.gpsimd.dma_start(gate_in[:], og[0])
+        nc.sync.dma_start(gate_in[:], og[0])
 
-        ks_g = sb.tile([P, N], U8, name="ks_g", align_bytes=64)
-        nc.vector.tensor_copy(ks_g[:], ks_pool[:].indirect(offsets[:]))
+        nc.vector.memset(ones[:], 1.0)
+        nc.vector.memset(ident[:], 0.0)
+        nc.vector.tensor_tensor_scan(ramp[:], ones[:], ones[:], 0.0, ALU.mult, ALU.add)
+        nc.vector.transpose(ramp_t[:], ramp[:])
+        nc.scalar.activation(distance[:], ramp[:], ACT.Abs, bias=ramp_t[:, 0:1], scale=-1.0)
+        for quad in range(4):
+            rows = slice(32 * quad, 32 * quad + 32)
+            nc.scalar.activation(ident[rows, rows], distance[rows, :], ACT.Relu, bias=ramp[rows, 0:1], scale=-1.0)
+
         vs_g = sb.tile([P, N], F32, name="vs_g", align_bytes=64)
         nc.vector.tensor_copy(vs_g[:], vs_pool[:].indirect(offsets[:]))
+        ks_g = sb.tile([P, N], U8, name="ks_g", align_bytes=64)
+        nc.vector.tensor_copy(ks_g[:], ks_pool[:].indirect(offsets[:]))
 
         neg = sb.tile([P, N + 1], F32, name="neg", tag="slot_c", align_bytes=64)
         nc.scalar.mul(neg[:, N : N + 1], sink_col[:], -1.0)

@@ -43,31 +43,31 @@ def tile_attend_soft_sink_gate_srtq128n512t2048_kernel(
         qw = sb.tile([P, NQ], U32, name="qw", align_bytes=64)
         qs = sb.tile([P, NQ], U8, name="qs", align_bytes=64)
         gate_in = sb.tile([P, DV], F32, name="gate_in")
+        sink_col = sb.tile([P, 1], F32, name="sink_col")
         ident = sb.tile([P, P], F32, name="ident", align_bytes=64)
-
         ones = sb.tile([P, 32], F32, name="ones", align_bytes=64)
         ramp = sb.tile([P, 32], F32, name="ramp", align_bytes=64)
         ramp_t = sb.tile([P, 32], F32, name="ramp_t", align_bytes=64)
         distance = sb.tile([P, 32], F32, name="distance", align_bytes=64)
 
+        nc.vector.memset(ones[:], 1.0)
         nc.vector.memset(ks_pool[:].bitcast(I32), 0)
+        nc.vector.tensor_tensor_scan(ramp[:], ones[:], ones[:], 0.0, ALU.mult, ALU.add)
         nc.vector.memset(qs[:].bitcast(I32), 0)
         nc.vector.memset(vs_pool[0:VS_ROW, :].bitcast(I32), 0)
+        nc.vector.transpose(ramp_t[:], ramp[:])
+
         q_rows = q_scales[0, 0].bitcast(I32)
         k_rows = k_scales[0].bitcast(I32)
         k_all = k_words[0].rearrange("p n t -> p (n t)").bitcast(I32)
 
-        def load_keys(first, last):
-            nc.sync.dma_start(kw_pool[:, first:last].bitcast(I32), k_all[:, first:last])
-
-        sink_col = sb.tile([P, 1], F32, name="sink_col")
         nc.sync.dma_start(offsets[:], offs)
         nc.scalar.dma_start(vs_pool[VS_ROW : VS_ROW + 1, :], vs[0:1, :])
-        load_keys(0, K_CUT)
+        nc.sync.dma_start(kw_pool[:, :K_CUT].bitcast(I32), k_all[:, :K_CUT])
         for quad in range(4):
             queue = nc.sync if quad < 3 else nc.scalar
             queue.dma_start(ks_pool[32 * quad : 32 * quad + 4, :].bitcast(I32), k_rows[4 * quad : 4 * quad + 4, :])
-        load_keys(K_CUT, T)
+        nc.sync.dma_start(kw_pool[:, K_CUT:].bitcast(I32), k_all[:, K_CUT:])
         nc.sync.dma_start(qw[:].bitcast(I32), q_words[0, 0].rearrange("p n t -> p (n t)").bitcast(I32))
         for quad in range(4):
             nc.sync.dma_start(qs[32 * quad : 32 * quad + 4, :].bitcast(I32), q_rows[4 * quad : 4 * quad + 4, :])
@@ -75,10 +75,7 @@ def tile_attend_soft_sink_gate_srtq128n512t2048_kernel(
         nc.sync.dma_start(v_pool[:], vT)
         nc.sync.dma_start(gate_in[:], og[0])
 
-        nc.vector.memset(ones[:], 1.0)
-        nc.vector.memset(ident[:], 0.0)
-        nc.vector.tensor_tensor_scan(ramp[:], ones[:], ones[:], 0.0, ALU.mult, ALU.add)
-        nc.vector.transpose(ramp_t[:], ramp[:])
+        nc.scalar.activation(ident[:], ones[:, 0:1].to_broadcast([P, P]), ACT.Copy, scale=0.0)
         nc.scalar.activation(distance[:], ramp[:], ACT.Abs, bias=ramp_t[:, 0:1], scale=-1.0)
         for quad in range(4):
             rows = slice(32 * quad, 32 * quad + 32)
@@ -89,13 +86,17 @@ def tile_attend_soft_sink_gate_srtq128n512t2048_kernel(
         ks_g = sb.tile([P, N], U8, name="ks_g", align_bytes=64)
         nc.vector.tensor_copy(ks_g[:], ks_pool[:].indirect(offsets[:]))
 
-        neg = sb.tile([P, N + 1], F32, name="neg", tag="slot_c", align_bytes=64)
+        vs_ps = ps.tile([P, PACK, P], F32, name="vs_ps")
+        for t in range(PACK):
+            nc.tensor.transpose(vs_ps[:, t, :], vs_g[:, t::PACK], ident[:])
+        vs_col = sb.tile([P, PACK], F32, name="vs_col", align_bytes=64)
+        nc.scalar.copy(vs_col[:], vs_ps[:, :, VS_ROW])
+
+        neg = sb.tile([P, N + 1], F32, name="neg", align_bytes=64)
         nc.scalar.mul(neg[:, N : N + 1], sink_col[:], -1.0)
-        vs_d = sb.tile([P, PACK, P], F32, name="vs_d", align_bytes=64)
-        nc.scalar.copy(vs_d[:], vs_g[:].rearrange("p (s t) -> p t s", t=PACK))
 
         kw_g = [sb.tile([P, HALF], U32, name=f"kw_g{h}", tag=("slot_a", "slot_b")[h], align_bytes=64) for h in range(2)]
-        scores = [ps.tile([P, HALF], F32, name=f"scores{h}", tag=f"bank{h}") for h in range(2)]
+        scores = [ps.tile([P, HALF], F32, name=f"scores{h}") for h in range(2)]
         for h in range(2):
             cols = HALF // 16
             nc.vector.tensor_copy(kw_g[h][:], kw_pool[:].indirect(offsets[:, h * cols : (h + 1) * cols]))
@@ -124,21 +125,17 @@ def tile_attend_soft_sink_gate_srtq128n512t2048_kernel(
             )
             start_value = neg_max[h][:]
 
-        vs_ps = ps.tile([P, PACK, P], F32, name="vs_ps", tag="bank0")
-        for t in range(PACK):
-            nc.tensor.transpose(vs_ps[:, t, :], vs_d[:, t, :], ident[:])
-
         p_sb = sb.tile([P, N + 1], F32, name="p_sb", align_bytes=64)
-        sums = [sb.tile([P, 1], F32, name=f"sums{h}") for h in range(2)]
+        sums = sb.tile([P, 4], F32, name="sums")
         p_ps = ps.tile([P, PACK, P], F32, name="p_ps")
-        for h in range(2):
-            cols = slice(h * HALF, (h + 1) * HALF + h)
-            nc.scalar.activation(p_sb[:, cols], neg[:, cols], ACT.Exp, bias=neg_max[1][:], scale=-1.0, accum_out=sums[h][:])
-            for t in (2 * h, 2 * h + 1):
+        for part in range(4):
+            width = N // 4
+            cols = slice(part * width, (part + 1) * width + (part == 4 - 1))
+            nc.scalar.activation(
+                p_sb[:, cols], neg[:, cols], ACT.Exp, bias=neg_max[1][:], scale=-1.0, accum_out=sums[:, part : part + 1]
+            )
+            for t in range(part * width // P, (part + 1) * width // P):
                 nc.tensor.transpose(p_ps[:, t, :], p_sb[:, t * P : (t + 1) * P], ident[:])
-
-        vs_col = sb.tile([P, PACK], F32, name="vs_col", tag="slot_c", align_bytes=64)
-        nc.scalar.copy(vs_col[:], vs_ps[:, :, VS_ROW])
 
         v_g = sb.tile([P, N], BF16, name="v_g", tag="slot_b", align_bytes=64)
         nc.vector.tensor_copy(v_g[:], v_pool[:].indirect(offsets[:]))
@@ -146,13 +143,11 @@ def tile_attend_soft_sink_gate_srtq128n512t2048_kernel(
         v_words = v_g[:].bitcast(F32)
         for u in range(2):
             nc.tensor.transpose(v_ps[:, u, :], v_words[:, u::2], ident[:])
+        total = sb.tile([P, 1], F32, name="total")
+        sums_copy = sb.tile([P, 4], F32, name="sums_copy")
+        nc.scalar.activation(sums_copy[:], sums[:], ACT.Identity, accum_out=total[:])
         v_q = sb.tile([P, DV, PACK], BF16, name="v_q", align_bytes=64)
         nc.scalar.copy(v_q[:].bitcast(F32), v_ps[:].rearrange("s u e -> s e u"))
-
-        total = sb.tile([P, 1], F32, name="total")
-        nc.scalar.activation(total[:], sums[0][:], ACT.Identity, bias=sums[1][:])
-        inv_total = sb.tile([P, 1], F32, name="inv_total")
-        nc.vector.reciprocal(inv_total[:], total[:])
 
         w_q = sb.tile([P, NQ, PACK], BF16, name="w_q", align_bytes=64)
         nc.vector.tensor_tensor(
@@ -161,6 +156,8 @@ def tile_attend_soft_sink_gate_srtq128n512t2048_kernel(
             vs_col[:].unsqueeze(1).broadcast_to([P, NQ, PACK]),
             ALU.mult,
         )
+        inv_total = sb.tile([P, 1], F32, name="inv_total", tag="slot_a", align_bytes=64)
+        nc.vector.reciprocal(inv_total[:], total[:])
 
         w_codes = sb.tile([P, NQ], U32, name="w_codes", align_bytes=64)
         w_scales = sb.tile([P, NQ], U8, name="w_scales", align_bytes=64)

@@ -65,8 +65,7 @@ def tile_attend_soft_sink_gate_srtq128n512t2048_kernel(
         nc.scalar.dma_start(vs_pool[VS_ROW : VS_ROW + 1, :], vs[0:1, :])
         nc.sync.dma_start(kw_pool[:, :K_CUT].bitcast(I32), k_all[:, :K_CUT])
         for quad in range(4):
-            queue = nc.sync if quad < 3 else nc.scalar
-            queue.dma_start(ks_pool[32 * quad : 32 * quad + 4, :].bitcast(I32), k_rows[4 * quad : 4 * quad + 4, :])
+            nc.sync.dma_start(ks_pool[32 * quad : 32 * quad + 4, :].bitcast(I32), k_rows[4 * quad : 4 * quad + 4, :])
         nc.sync.dma_start(kw_pool[:, K_CUT:].bitcast(I32), k_all[:, K_CUT:])
         nc.sync.dma_start(qw[:].bitcast(I32), q_words[0, 0].rearrange("p n t -> p (n t)").bitcast(I32))
         for quad in range(4):
@@ -92,7 +91,7 @@ def tile_attend_soft_sink_gate_srtq128n512t2048_kernel(
         vs_col = sb.tile([P, PACK], F32, name="vs_col", align_bytes=64)
         nc.scalar.copy(vs_col[:], vs_ps[:, :, VS_ROW])
 
-        neg = sb.tile([P, N + 1], F32, name="neg", align_bytes=64)
+        neg = sb.tile([P, N + 1], F32, name="neg", tag="slot_d", align_bytes=64)
         nc.scalar.mul(neg[:, N : N + 1], sink_col[:], -1.0)
 
         kw_g = [sb.tile([P, HALF], U32, name=f"kw_g{h}", tag=("slot_a", "slot_b")[h], align_bytes=64) for h in range(2)]
@@ -146,6 +145,10 @@ def tile_attend_soft_sink_gate_srtq128n512t2048_kernel(
         total = sb.tile([P, 1], F32, name="total")
         sums_copy = sb.tile([P, 4], F32, name="sums_copy")
         nc.scalar.activation(sums_copy[:], sums[:], ACT.Identity, accum_out=total[:])
+        half_tanh = sb.tile([P, DV], F32, name="half_tanh", tag="slot_d", align_bytes=64)
+        nc.scalar.activation(half_tanh[:], gate_in[:], ACT.Tanh, scale=0.5)
+        gate = sb.tile([P, DV], F32, name="gate")
+        nc.scalar.activation(gate[:], half_tanh[:], ACT.Copy, bias=0.5, scale=0.5)
         v_q = sb.tile([P, DV, PACK], BF16, name="v_q", align_bytes=64)
         nc.scalar.copy(v_q[:].bitcast(F32), v_ps[:].rearrange("s u e -> s e u"))
 
@@ -169,11 +172,6 @@ def tile_attend_soft_sink_gate_srtq128n512t2048_kernel(
         nc.vector.quantize_mx(
             out=v_codes[:].bitcast(FP8X4), scales=v_scales[:], in_=v_q[:].rearrange("s e t -> s (e t)")
         )
-
-        half_tanh = sb.tile([P, DV], F32, name="half_tanh", tag="slot_b", align_bytes=64)
-        nc.scalar.activation(half_tanh[:], gate_in[:], ACT.Tanh, scale=0.5)
-        gate = sb.tile([P, DV], F32, name="gate")
-        nc.scalar.activation(gate[:], half_tanh[:], ACT.Copy, bias=0.5, scale=0.5)
 
         y_ps = ps.tile([P, DV], F32, name="y_ps")
         nc.tensor.matmul_mx(

@@ -53,9 +53,9 @@ def tile_attend_soft_sink_gate_srtq128n512t2048_kernel(
         nc.vector.memset(ones[:], 1.0)
         nc.vector.memset(ks_pool[:].bitcast(I32), 0)
         nc.vector.tensor_tensor_scan(ramp[:], ones[:], ones[:], 0.0, ALU.mult, ALU.add)
-        nc.vector.memset(qs[:].bitcast(I32), 0)
         nc.vector.memset(vs_pool[0:VS_ROW, :].bitcast(I32), 0)
         nc.vector.transpose(ramp_t[:], ramp[:])
+        nc.vector.memset(qs[:].bitcast(I32), 0)
 
         q_rows = q_scales[0, 0].bitcast(I32)
         k_rows = k_scales[0].bitcast(I32)
@@ -150,7 +150,9 @@ def tile_attend_soft_sink_gate_srtq128n512t2048_kernel(
         gate = sb.tile([P, DV], F32, name="gate")
         nc.scalar.activation(gate[:], half_tanh[:], ACT.Copy, bias=0.5, scale=0.5)
         v_q = sb.tile([P, DV, PACK], BF16, name="v_q", align_bytes=64)
-        nc.scalar.copy(v_q[:].bitcast(F32), v_ps[:].rearrange("s u e -> s e u"))
+        for g in range(2):
+            cols = slice(g * DV // 2, (g + 1) * DV // 2)
+            nc.scalar.copy(v_q[:, cols, :].bitcast(F32), v_ps[:, :, cols].rearrange("s u e -> s e u"))
 
         w_q = sb.tile([P, NQ, PACK], BF16, name="w_q", align_bytes=64)
         nc.vector.tensor_tensor(
@@ -169,20 +171,25 @@ def tile_attend_soft_sink_gate_srtq128n512t2048_kernel(
         )
         v_codes = sb.tile([P, DV], U32, name="v_codes", align_bytes=64)
         v_scales = sb.tile([P, DV], U8, name="v_scales", align_bytes=64)
-        nc.vector.quantize_mx(
-            out=v_codes[:].bitcast(FP8X4), scales=v_scales[:], in_=v_q[:].rearrange("s e t -> s (e t)")
-        )
-
-        y_ps = ps.tile([P, DV], F32, name="y_ps")
-        nc.tensor.matmul_mx(
-            out=y_ps[:],
-            lhsT=w_codes[:].bitcast(FP8X4),
-            lhsT_scale=w_scales[:],
-            rhs=v_codes[:].bitcast(FP8X4),
-            rhs_scale=v_scales[:],
-            start=True,
-            stop=True,
-        )
         y = sb.tile([P, DV], F32, name="y")
-        nc.vector.scalar_tensor_tensor(y[:], y_ps[:], inv_total[:], gate[:], ALU.mult, ALU.mult)
+        y_ps = [ps.tile([P, DV // 2], F32, name=f"y_ps{g}") for g in range(2)]
+        for g in range(2):
+            cols = slice(g * DV // 2, (g + 1) * DV // 2)
+            nc.vector.quantize_mx(
+                out=v_codes[:, cols].bitcast(FP8X4),
+                scales=v_scales[:, cols],
+                in_=v_q[:, cols, :].rearrange("s e t -> s (e t)"),
+            )
+            nc.tensor.matmul_mx(
+                out=y_ps[g][:],
+                lhsT=w_codes[:].bitcast(FP8X4),
+                lhsT_scale=w_scales[:],
+                rhs=v_codes[:, cols].bitcast(FP8X4),
+                rhs_scale=v_scales[:, cols],
+                start=True,
+                stop=True,
+            )
+        for g in range(2):
+            cols = slice(g * DV // 2, (g + 1) * DV // 2)
+            nc.vector.scalar_tensor_tensor(y[:, cols], y_ps[g][:], inv_total[:], gate[:, cols], ALU.mult, ALU.mult)
         nc.sync.dma_start(out[0], y[:])

@@ -11,7 +11,10 @@ D = 512
 PACK = 4
 HALF = N // 2
 VS_ROW = P - 1
-K_CUT = 640
+K_CUT = 448
+PREFIX = T - HALF
+PERIOD = 14
+REPEATS = 5
 
 FLOPS = 2 * NQ * N * D + 2 * NQ * N * DV
 BYTES = P * T * 4 + 16 * T + P * NQ * 4 + 16 * NQ + DV * T * 4 + T * 4 + NQ * 4 + 2 * NQ * DV * 4 + P * (N // 16) * 2
@@ -43,19 +46,20 @@ def tile_attend_soft_sink_gate_srtq128n512t2048_kernel(
         qw = sb.tile([P, NQ], U32, name="qw", align_bytes=64)
         qs = sb.tile([P, NQ], U8, name="qs", align_bytes=64)
         gate_in = sb.tile([P, DV], F32, name="gate_in")
-        sink_col = sb.tile([P, 1], F32, name="sink_col")
+        vs_g = sb.tile([P, N], F32, name="vs_g", align_bytes=64)
+        sink_col = vs_g[:, HALF : HALF + 1]
         ident = sb.tile([P, P], F32, name="ident", align_bytes=64)
         ones = sb.tile([P, 32], F32, name="ones", align_bytes=64)
         ramp = sb.tile([P, 32], F32, name="ramp", align_bytes=64)
         ramp_t = sb.tile([P, 32], F32, name="ramp_t", align_bytes=64)
         distance = sb.tile([P, 32], F32, name="distance", align_bytes=64)
 
-        nc.vector.memset(ones[:], 1.0)
         nc.vector.memset(ks_pool[:].bitcast(I32), 0)
+        nc.vector.memset(ones[:], 1.0)
+        nc.vector.memset(qs[:].bitcast(I32), 0)
         nc.vector.tensor_tensor_scan(ramp[:], ones[:], ones[:], 0.0, ALU.mult, ALU.add)
         nc.vector.memset(vs_pool[0:VS_ROW, :].bitcast(I32), 0)
         nc.vector.transpose(ramp_t[:], ramp[:])
-        nc.vector.memset(qs[:].bitcast(I32), 0)
 
         q_rows = q_scales[0, 0].bitcast(I32)
         k_rows = k_scales[0].bitcast(I32)
@@ -66,11 +70,15 @@ def tile_attend_soft_sink_gate_srtq128n512t2048_kernel(
         nc.sync.dma_start(kw_pool[:, :K_CUT].bitcast(I32), k_all[:, :K_CUT])
         for quad in range(4):
             nc.sync.dma_start(ks_pool[32 * quad : 32 * quad + 4, :].bitcast(I32), k_rows[4 * quad : 4 * quad + 4, :])
-        nc.sync.dma_start(kw_pool[:, K_CUT:].bitcast(I32), k_all[:, K_CUT:])
+        nc.sync.dma_start(kw_pool[:, K_CUT:PREFIX].bitcast(I32), k_all[:, K_CUT:PREFIX])
+        nc.sync.dma_start(
+            qs[0 : REPEATS * PERIOD, :].bitcast(I32),
+            q_rows[0:PERIOD, :].unsqueeze(0).broadcast_to([REPEATS, PERIOD, NQ // 4]),
+        )
+        nc.sync.dma_start(qs[96:100, :].bitcast(I32), q_rows[12:16, :])
+        nc.sync.dma_start(kw_pool[:, PREFIX:].bitcast(I32), k_all[:, PREFIX:])
         nc.sync.dma_start(qw[:].bitcast(I32), q_words[0, 0].rearrange("p n t -> p (n t)").bitcast(I32))
-        for quad in range(4):
-            nc.sync.dma_start(qs[32 * quad : 32 * quad + 4, :].bitcast(I32), q_rows[4 * quad : 4 * quad + 4, :])
-        nc.sync.dma_start(sink_col[:], sink[0])
+        nc.sync.dma_start(sink_col, sink[0])
         nc.sync.dma_start(v_pool[:], vT)
         nc.sync.dma_start(gate_in[:], og[0])
 
@@ -80,27 +88,25 @@ def tile_attend_soft_sink_gate_srtq128n512t2048_kernel(
             rows = slice(32 * quad, 32 * quad + 32)
             nc.scalar.activation(ident[rows, rows], distance[rows, :], ACT.Relu, bias=ramp[rows, 0:1], scale=-1.0)
 
-        vs_g = sb.tile([P, N], F32, name="vs_g", align_bytes=64)
-        nc.vector.tensor_copy(vs_g[:], vs_pool[:].indirect(offsets[:]))
+        cols = HALF // 16
+
+        def gather_vs(h):
+            slots = slice(h * HALF, (h + 1) * HALF)
+            nc.vector.tensor_copy(vs_g[:, slots], vs_pool[:].indirect(offsets[:, h * cols : (h + 1) * cols]))
+
+        gather_vs(0)
         ks_g = sb.tile([P, N], U8, name="ks_g", align_bytes=64)
         nc.vector.tensor_copy(ks_g[:], ks_pool[:].indirect(offsets[:]))
 
-        vs_ps = ps.tile([P, PACK, P], F32, name="vs_ps")
-        for t in range(PACK):
-            nc.tensor.transpose(vs_ps[:, t, :], vs_g[:, t::PACK], ident[:])
-        vs_col = sb.tile([P, PACK], F32, name="vs_col", align_bytes=64)
-        nc.scalar.copy(vs_col[:], vs_ps[:, :, VS_ROW])
-
         neg = sb.tile([P, N + 1], F32, name="neg", tag="slot_d", align_bytes=64)
-        nc.scalar.mul(neg[:, N : N + 1], sink_col[:], -1.0)
+        nc.scalar.mul(neg[:, N : N + 1], sink_col, -1.0)
 
-        kw_g = [sb.tile([P, HALF], U32, name=f"kw_g{h}", tag=("slot_a", "slot_b")[h], align_bytes=64) for h in range(2)]
-        scores = [ps.tile([P, HALF], F32, name=f"scores{h}") for h in range(2)]
+        kw_g = [sb.tile([P, HALF], U32, name=f"kw_g{h}", tag=("kw_g0", "kw_g1")[h], align_bytes=64) for h in range(2)]
+        scores = ps.tile([P, N], F32, name="scores")
         for h in range(2):
-            cols = HALF // 16
-            nc.vector.tensor_copy(kw_g[h][:], kw_pool[:].indirect(offsets[:, h * cols : (h + 1) * cols]))
+            nc.vector.tensor_copy(kw_g[h][:], kw_pool[:, : (PREFIX, T)[h]].indirect(offsets[:, h * cols : (h + 1) * cols]))
             nc.tensor.matmul_mx(
-                out=scores[h][:],
+                out=scores[:, h * HALF : (h + 1) * HALF],
                 lhsT=qw[:].bitcast(FP8X4),
                 lhsT_scale=qs[:],
                 rhs=kw_g[h][:].bitcast(FP8X4),
@@ -109,20 +115,21 @@ def tile_attend_soft_sink_gate_srtq128n512t2048_kernel(
                 stop=True,
             )
 
-        neg_dealt = neg[:, 0:N].rearrange("q (t s) -> q t s", t=PACK)
-        neg_max = [sb.tile([P, 1], F32, name=f"neg_max{h}") for h in range(2)]
-        start_value = neg[:, N : N + 1]
-        for h in range(2):
-            nc.vector.tensor_scalar(
-                neg_dealt[:, :, h * 64 : (h + 1) * 64],
-                scores[h][:].rearrange("q (s t) -> q t s", t=PACK),
-                -1.0,
-                start_value,
-                ALU.mult,
-                ALU.min,
-                accum_out=neg_max[h][:],
-            )
-            start_value = neg_max[h][:]
+        gather_vs(1)
+        neg_max = sb.tile([P, 1], F32, name="neg_max")
+        nc.vector.tensor_scalar(
+            neg[:, 0:N].rearrange("q (t s) -> q t s", t=PACK),
+            scores[:].rearrange("q (s t) -> q t s", t=PACK),
+            -1.0,
+            neg[:, N : N + 1],
+            ALU.mult,
+            ALU.min,
+            accum_out=neg_max[:],
+        )
+
+        vs_ps = ps.tile([P, PACK, P], F32, name="vs_ps")
+        for t in range(PACK):
+            nc.tensor.transpose(vs_ps[:, t, :], vs_g[:, t::PACK], ident[:])
 
         p_sb = sb.tile([P, N + 1], F32, name="p_sb", align_bytes=64)
         sums = sb.tile([P, 4], F32, name="sums")
@@ -131,7 +138,7 @@ def tile_attend_soft_sink_gate_srtq128n512t2048_kernel(
             width = N // 4
             cols = slice(part * width, (part + 1) * width + (part == 4 - 1))
             nc.scalar.activation(
-                p_sb[:, cols], neg[:, cols], ACT.Exp, bias=neg_max[1][:], scale=-1.0, accum_out=sums[:, part : part + 1]
+                p_sb[:, cols], neg[:, cols], ACT.Exp, bias=neg_max[:], scale=-1.0, accum_out=sums[:, part : part + 1]
             )
             for t in range(part * width // P, (part + 1) * width // P):
                 nc.tensor.transpose(p_ps[:, t, :], p_sb[:, t * P : (t + 1) * P], ident[:])
@@ -142,10 +149,12 @@ def tile_attend_soft_sink_gate_srtq128n512t2048_kernel(
         v_words = v_g[:].bitcast(F32)
         for u in range(2):
             nc.tensor.transpose(v_ps[:, u, :], v_words[:, u::2], ident[:])
+        vs_col = sb.tile([P, PACK], F32, name="vs_col", tag="slot_d", align_bytes=64)
+        nc.scalar.copy(vs_col[:], vs_ps[:, :, VS_ROW])
         total = sb.tile([P, 1], F32, name="total")
         sums_copy = sb.tile([P, 4], F32, name="sums_copy")
         nc.scalar.activation(sums_copy[:], sums[:], ACT.Identity, accum_out=total[:])
-        half_tanh = sb.tile([P, DV], F32, name="half_tanh", tag="slot_d", align_bytes=64)
+        half_tanh = sb.tile([P, DV], F32, name="half_tanh", align_bytes=64)
         nc.scalar.activation(half_tanh[:], gate_in[:], ACT.Tanh, scale=0.5)
         gate = sb.tile([P, DV], F32, name="gate")
         nc.scalar.activation(gate[:], half_tanh[:], ACT.Copy, bias=0.5, scale=0.5)

@@ -36,38 +36,38 @@ def tile_attend_soft_sink_gate_srtq128n512t2048_kernel(
     nc = tc.nc
     with ExitStack() as ctx:
         sb = ctx.enter_context(tc.tile_pool(name="sb", bufs=1))
+        reuse = ctx.enter_context(tc.tile_pool(name="reuse", bufs=1))
         ps = ctx.enter_context(tc.psum_pool(name="ps", bufs=1))
 
         offsets = sb.tile([P, N // 16], U16, name="offsets")
         kw_pool = sb.tile([P, T], U32, name="kw_pool", align_bytes=64)
-        ks_pool = sb.tile([P, T], U8, name="ks_pool", tag="slot_a", align_bytes=64)
-        v_pool = sb.tile([P, T], F32, name="v_pool", align_bytes=64)
-        vs_pool = sb.tile([P, T], F32, name="vs_pool", tag="slot_b", align_bytes=64)
+        ks_pool = sb.tile([P, T], U8, name="ks_pool", align_bytes=64)
+        v_pool = reuse.tile([P, T], F32, name="v_pool", offset=0, align_bytes=64)
+        vs_pool = sb.tile([P, T], F32, name="vs_pool", align_bytes=64)
         qw = sb.tile([P, NQ], U32, name="qw", align_bytes=64)
         qs = sb.tile([P, NQ], U8, name="qs", align_bytes=64)
         gate_in = sb.tile([P, DV], F32, name="gate_in")
-        vs_g = sb.tile([P, N], F32, name="vs_g", align_bytes=64)
-        sink_col = vs_g[:, HALF : HALF + 1]
-        ident = sb.tile([P, P], F32, name="ident", align_bytes=64)
-        ones = sb.tile([P, 32], F32, name="ones", align_bytes=64)
-        ramp = sb.tile([P, 32], F32, name="ramp", align_bytes=64)
+        sink_col = sb.tile([P, 1], F32, name="sink_col")
+        ones = sb.tile([P, P], F32, name="ones", align_bytes=64)
+        ramp = sb.tile([P, P], F32, name="ramp", tag="ramp", align_bytes=64)
         ramp_t = sb.tile([P, 32], F32, name="ramp_t", align_bytes=64)
-        distance = sb.tile([P, 32], F32, name="distance", align_bytes=64)
+        first_lane = sb.tile([P, 1], F32, name="first_lane")
+        ident = sb.tile([P, P], F32, name="ident", align_bytes=64)
 
         nc.vector.memset(ks_pool[:].bitcast(I32), 0)
         nc.vector.memset(ones[:], 1.0)
         nc.vector.memset(qs[:].bitcast(I32), 0)
         nc.vector.tensor_tensor_scan(ramp[:], ones[:], ones[:], 0.0, ALU.mult, ALU.add)
         nc.vector.memset(vs_pool[0:VS_ROW, :].bitcast(I32), 0)
-        nc.vector.transpose(ramp_t[:], ramp[:])
+        nc.vector.transpose(ramp_t[:], ramp[:, :32])
 
         q_rows = q_scales[0, 0].bitcast(I32)
         k_rows = k_scales[0].bitcast(I32)
         k_all = k_words[0].rearrange("p n t -> p (n t)").bitcast(I32)
 
-        nc.sync.dma_start(offsets[:], offs)
         nc.scalar.dma_start(vs_pool[VS_ROW : VS_ROW + 1, :], vs[0:1, :])
         nc.sync.dma_start(kw_pool[:, :K_CUT].bitcast(I32), k_all[:, :K_CUT])
+        nc.sync.dma_start(offsets[:], offs)
         for quad in range(4):
             nc.sync.dma_start(ks_pool[32 * quad : 32 * quad + 4, :].bitcast(I32), k_rows[4 * quad : 4 * quad + 4, :])
         nc.sync.dma_start(kw_pool[:, K_CUT:PREFIX].bitcast(I32), k_all[:, K_CUT:PREFIX])
@@ -75,120 +75,129 @@ def tile_attend_soft_sink_gate_srtq128n512t2048_kernel(
             qs[0 : REPEATS * PERIOD, :].bitcast(I32),
             q_rows[0:PERIOD, :].unsqueeze(0).broadcast_to([REPEATS, PERIOD, NQ // 4]),
         )
-        nc.sync.dma_start(qs[96:100, :].bitcast(I32), q_rows[12:16, :])
         nc.sync.dma_start(kw_pool[:, PREFIX:].bitcast(I32), k_all[:, PREFIX:])
         nc.sync.dma_start(qw[:].bitcast(I32), q_words[0, 0].rearrange("p n t -> p (n t)").bitcast(I32))
-        nc.sync.dma_start(sink_col, sink[0])
+        nc.sync.dma_start(qs[96:100, :].bitcast(I32), q_rows[12:16, :])
+        nc.sync.dma_start(sink_col[:], sink[0])
         nc.sync.dma_start(v_pool[:], vT)
         nc.sync.dma_start(gate_in[:], og[0])
 
-        nc.scalar.activation(ident[:], ones[:, 0:1].to_broadcast([P, P]), ACT.Copy, scale=0.0)
-        nc.scalar.activation(distance[:], ramp[:], ACT.Abs, bias=ramp_t[:, 0:1], scale=-1.0)
         for quad in range(4):
             rows = slice(32 * quad, 32 * quad + 32)
-            nc.scalar.activation(ident[rows, rows], distance[rows, :], ACT.Relu, bias=ramp[rows, 0:1], scale=-1.0)
+            nc.scalar.activation(first_lane[rows, :], ones[rows, 0:1], ACT.Copy, scale=32.0 * quad)
+        nc.vector.tensor_scalar(ident[:], ramp[:], first_lane[:], ramp_t[:, 0:1], ALU.subtract, ALU.is_equal)
 
-        cols = HALF // 16
+        def listed(pool, first, last):
+            return pool.indirect(offsets[:, first // 16 : last // 16])
 
-        def gather_vs(h):
-            slots = slice(h * HALF, (h + 1) * HALF)
-            nc.vector.tensor_copy(vs_g[:, slots], vs_pool[:].indirect(offsets[:, h * cols : (h + 1) * cols]))
+        vs_g = sb.tile([P, N], F32, name="vs_g", align_bytes=64)
+        nc.scalar.activation(vs_g[:], listed(vs_pool[:], 0, N), ACT.Copy)
+        vs_ps = ps.tile([P, PACK, P], F32, name="vs_ps")
+        for t in range(PACK):
+            nc.tensor.transpose(vs_ps[:, t, :], vs_g[:, t::PACK], ident[:])
+        vs_col = sb.tile([P, PACK], F32, name="vs_col")
+        nc.scalar.copy(vs_col[:], vs_ps[:, :, VS_ROW])
 
-        gather_vs(0)
-        ks_g = sb.tile([P, N], U8, name="ks_g", align_bytes=64)
-        nc.vector.tensor_copy(ks_g[:], ks_pool[:].indirect(offsets[:]))
+        ks_g = sb.tile([P, N], U8, name="ks_g", tag="ramp", align_bytes=64)
+        nc.vector.tensor_copy(ks_g[:], listed(ks_pool[:], 0, N))
 
-        neg = sb.tile([P, N + 1], F32, name="neg", tag="slot_d", align_bytes=64)
-        nc.scalar.mul(neg[:, N : N + 1], sink_col, -1.0)
+        neg = sb.tile([P, N + 1], F32, name="neg", align_bytes=64)
+        nc.scalar.mul(neg[:, N : N + 1], sink_col[:], -1.0)
 
-        kw_g = [sb.tile([P, HALF], U32, name=f"kw_g{h}", tag=("kw_g0", "kw_g1")[h], align_bytes=64) for h in range(2)]
-        scores = ps.tile([P, N], F32, name="scores")
+        scores = [ps.tile([P, HALF], F32, name=f"scores{h}") for h in range(2)]
         for h in range(2):
-            nc.vector.tensor_copy(kw_g[h][:], kw_pool[:, : (PREFIX, T)[h]].indirect(offsets[:, h * cols : (h + 1) * cols]))
+            kw_g = sb.tile([P, HALF], U32, name=f"kw_g{h}", align_bytes=64)
+            nc.vector.tensor_copy(kw_g[:], listed(kw_pool[:, : (PREFIX, T)[h]], h * HALF, (h + 1) * HALF))
             nc.tensor.matmul_mx(
-                out=scores[:, h * HALF : (h + 1) * HALF],
+                out=scores[h][:],
                 lhsT=qw[:].bitcast(FP8X4),
                 lhsT_scale=qs[:],
-                rhs=kw_g[h][:].bitcast(FP8X4),
+                rhs=kw_g[:].bitcast(FP8X4),
                 rhs_scale=ks_g[:, h * HALF : (h + 1) * HALF],
                 start=True,
                 stop=True,
             )
 
-        gather_vs(1)
-        neg_max = sb.tile([P, 1], F32, name="neg_max")
-        nc.vector.tensor_scalar(
-            neg[:, 0:N].rearrange("q (t s) -> q t s", t=PACK),
-            scores[:].rearrange("q (s t) -> q t s", t=PACK),
-            -1.0,
-            neg[:, N : N + 1],
-            ALU.mult,
-            ALU.min,
-            accum_out=neg_max[:],
-        )
-
-        vs_ps = ps.tile([P, PACK, P], F32, name="vs_ps")
-        for t in range(PACK):
-            nc.tensor.transpose(vs_ps[:, t, :], vs_g[:, t::PACK], ident[:])
+        planes = neg[:, 0:N].rearrange("q (t s) -> q t s", t=PACK)
+        half_max = sb.tile([P, 1], F32, name="half_max")
+        row_max = sb.tile([P, 1], F32, name="row_max")
+        neg_max = neg[:, N : N + 1]
+        for h in range(2):
+            so_far = neg_max
+            neg_max = (half_max[:], row_max[:])[h]
+            nc.vector.tensor_scalar(
+                planes[:, :, h * P // 2 : (h + 1) * P // 2],
+                scores[h][:].rearrange("q (s t) -> q t s", t=PACK),
+                -1.0,
+                so_far,
+                ALU.mult,
+                ALU.min,
+                accum_out=neg_max,
+            )
 
         p_sb = sb.tile([P, N + 1], F32, name="p_sb", align_bytes=64)
-        sums = sb.tile([P, 4], F32, name="sums")
         p_ps = ps.tile([P, PACK, P], F32, name="p_ps")
-        for part in range(4):
-            width = N // 4
-            cols = slice(part * width, (part + 1) * width + (part == 4 - 1))
-            nc.scalar.activation(
-                p_sb[:, cols], neg[:, cols], ACT.Exp, bias=neg_max[:], scale=-1.0, accum_out=sums[:, part : part + 1]
-            )
-            for t in range(part * width // P, (part + 1) * width // P):
-                nc.tensor.transpose(p_ps[:, t, :], p_sb[:, t * P : (t + 1) * P], ident[:])
+        for t in range(PACK):
+            cols = slice(t * P, (t + 1) * P + (t == PACK - 1))
+            nc.scalar.activation(p_sb[:, cols], neg[:, cols], ACT.Exp, bias=neg_max, scale=-1.0)
+            nc.tensor.transpose(p_ps[:, t, :], p_sb[:, t * P : (t + 1) * P], ident[:])
 
-        v_g = sb.tile([P, N], BF16, name="v_g", tag="slot_b", align_bytes=64)
-        nc.vector.tensor_copy(v_g[:], v_pool[:].indirect(offsets[:]))
-        v_ps = ps.tile([P, 2, DV], F32, name="v_ps")
+        v_g = sb.tile([P, N], BF16, name="v_g", align_bytes=64)
         v_words = v_g[:].bitcast(F32)
-        for u in range(2):
-            nc.tensor.transpose(v_ps[:, u, :], v_words[:, u::2], ident[:])
-        vs_col = sb.tile([P, PACK], F32, name="vs_col", tag="slot_d", align_bytes=64)
-        nc.scalar.copy(vs_col[:], vs_ps[:, :, VS_ROW])
+        nc.vector.tensor_copy(v_g[:], listed(v_pool[:], 0, N))
+        w_q = reuse.tile([P, NQ, PACK], BF16, name="w_q", offset=0, align_bytes=64)
+        for g in range(2):
+            queries = slice(g * NQ // 2, (g + 1) * NQ // 2)
+            nc.vector.tensor_tensor(
+                w_q[:, queries, :],
+                p_ps[:, :, queries].rearrange("s t q -> s q t"),
+                vs_col[:].unsqueeze(1).broadcast_to([P, NQ // 2, PACK]),
+                ALU.mult,
+            )
+        summed = sb.tile([P, N + 1], F32, name="summed", align_bytes=64)
         total = sb.tile([P, 1], F32, name="total")
-        sums_copy = sb.tile([P, 4], F32, name="sums_copy")
-        nc.scalar.activation(sums_copy[:], sums[:], ACT.Identity, accum_out=total[:])
+        nc.scalar.activation(summed[:], p_sb[:], ACT.Identity, accum_out=total[:])
         half_tanh = sb.tile([P, DV], F32, name="half_tanh", align_bytes=64)
         nc.scalar.activation(half_tanh[:], gate_in[:], ACT.Tanh, scale=0.5)
-        gate = sb.tile([P, DV], F32, name="gate")
-        nc.scalar.activation(gate[:], half_tanh[:], ACT.Copy, bias=0.5, scale=0.5)
+        v_ps = ps.tile([P, 2, DV], F32, name="v_ps")
+        for u in range(2):
+            nc.tensor.transpose(v_ps[:, u, :], v_words[:, u::2], ident[:])
         v_q = sb.tile([P, DV, PACK], BF16, name="v_q", align_bytes=64)
         for g in range(2):
             cols = slice(g * DV // 2, (g + 1) * DV // 2)
             nc.scalar.copy(v_q[:, cols, :].bitcast(F32), v_ps[:, :, cols].rearrange("s u e -> s e u"))
 
-        w_q = sb.tile([P, NQ, PACK], BF16, name="w_q", align_bytes=64)
-        nc.vector.tensor_tensor(
-            w_q[:],
-            p_ps[:].rearrange("s t q -> s q t"),
-            vs_col[:].unsqueeze(1).broadcast_to([P, NQ, PACK]),
-            ALU.mult,
-        )
-        inv_total = sb.tile([P, 1], F32, name="inv_total", tag="slot_a", align_bytes=64)
-        nc.vector.reciprocal(inv_total[:], total[:])
+        gate = sb.tile([P, DV], F32, name="gate")
+        nc.scalar.activation(gate[:], half_tanh[:], ACT.Copy, bias=0.5, scale=0.5)
 
         w_codes = sb.tile([P, NQ], U32, name="w_codes", align_bytes=64)
         w_scales = sb.tile([P, NQ], U8, name="w_scales", align_bytes=64)
-        nc.vector.quantize_mx(
-            out=w_codes[:].bitcast(FP8X4), scales=w_scales[:], in_=w_q[:].rearrange("s q t -> s (q t)")
-        )
         v_codes = sb.tile([P, DV], U32, name="v_codes", align_bytes=64)
         v_scales = sb.tile([P, DV], U8, name="v_scales", align_bytes=64)
         y = sb.tile([P, DV], F32, name="y")
         y_ps = [ps.tile([P, DV // 2], F32, name=f"y_ps{g}") for g in range(2)]
-        for g in range(2):
+
+        def quantise_values(g):
             cols = slice(g * DV // 2, (g + 1) * DV // 2)
             nc.vector.quantize_mx(
                 out=v_codes[:, cols].bitcast(FP8X4),
                 scales=v_scales[:, cols],
                 in_=v_q[:, cols, :].rearrange("s e t -> s (e t)"),
             )
+
+        for g in range(2):
+            queries = slice(g * NQ // 2, (g + 1) * NQ // 2)
+            nc.vector.quantize_mx(
+                out=w_codes[:, queries].bitcast(FP8X4),
+                scales=w_scales[:, queries],
+                in_=w_q[:, queries, :].rearrange("s q t -> s (q t)"),
+            )
+        quantise_values(0)
+        quantise_values(1)
+        inv_total = reuse.tile([P, 1], F32, name="inv_total", offset=2 * N, align_bytes=64)
+        nc.vector.reciprocal(inv_total[:], total[:])
+        for g in range(2):
+            cols = slice(g * DV // 2, (g + 1) * DV // 2)
             nc.tensor.matmul_mx(
                 out=y_ps[g][:],
                 lhsT=w_codes[:].bitcast(FP8X4),

@@ -15,6 +15,8 @@ K_CUT = 448
 PREFIX = T - HALF
 PERIOD = 14
 REPEATS = 5
+BLOCKS = N // 32
+RUN = 16
 
 FLOPS = 2 * NQ * N * D + 2 * NQ * N * DV
 BYTES = P * T * 4 + 16 * T + P * NQ * 4 + 16 * NQ + DV * T * 4 + T * 4 + NQ * 4 + 2 * NQ * DV * 4 + P * (N // 16) * 2
@@ -79,7 +81,8 @@ def tile_attend_soft_sink_gate_srtq128n512t2048_kernel(
         nc.sync.dma_start(qw[:].bitcast(I32), q_words[0, 0].rearrange("p n t -> p (n t)").bitcast(I32))
         nc.sync.dma_start(qs[96:100, :].bitcast(I32), q_rows[12:16, :])
         nc.sync.dma_start(sink_col[:], sink[0])
-        nc.sync.dma_start(v_pool[:], vT)
+        nc.sync.dma_start(v_pool[:, :PREFIX], vT[:, :PREFIX])
+        nc.sync.dma_start(v_pool[:, PREFIX:], vT[:, PREFIX:])
         nc.sync.dma_start(gate_in[:], og[0])
 
         for quad in range(4):
@@ -92,9 +95,14 @@ def tile_attend_soft_sink_gate_srtq128n512t2048_kernel(
 
         vs_g = sb.tile([P, N], F32, name="vs_g", align_bytes=64)
         nc.scalar.activation(vs_g[:], listed(vs_pool[:], 0, N), ACT.Copy)
+        vs_planes = sb.tile([P, PACK, P], F32, name="vs_planes", align_bytes=64)
+        nc.scalar.copy(
+            vs_planes[:].rearrange("p (u e) (b j) -> p u e b j", u=2, b=BLOCKS),
+            vs_g[:].rearrange("p (b u j e) -> p u e b j", b=BLOCKS, u=2, e=2),
+        )
         vs_ps = ps.tile([P, PACK, P], F32, name="vs_ps")
         for t in range(PACK):
-            nc.tensor.transpose(vs_ps[:, t, :], vs_g[:, t::PACK], ident[:])
+            nc.tensor.transpose(vs_ps[:, t, :], vs_planes[:, t, :], ident[:])
         vs_col = sb.tile([P, PACK], F32, name="vs_col")
         nc.scalar.copy(vs_col[:], vs_ps[:, :, VS_ROW])
 
@@ -118,7 +126,7 @@ def tile_attend_soft_sink_gate_srtq128n512t2048_kernel(
                 stop=True,
             )
 
-        planes = neg[:, 0:N].rearrange("q (t s) -> q t s", t=PACK)
+        by_parity = neg[:, 0:N].rearrange("q (e w) -> q e w", e=2)
         half_max = sb.tile([P, 1], F32, name="half_max")
         row_max = sb.tile([P, 1], F32, name="row_max")
         neg_max = neg[:, N : N + 1]
@@ -126,8 +134,8 @@ def tile_attend_soft_sink_gate_srtq128n512t2048_kernel(
             so_far = neg_max
             neg_max = (half_max[:], row_max[:])[h]
             nc.vector.tensor_scalar(
-                planes[:, :, h * P // 2 : (h + 1) * P // 2],
-                scores[h][:].rearrange("q (s t) -> q t s", t=PACK),
+                by_parity[:, :, h * P : (h + 1) * P],
+                scores[h][:].rearrange("q (w e) -> q e w", e=2),
                 -1.0,
                 so_far,
                 ALU.mult,
@@ -135,16 +143,27 @@ def tile_attend_soft_sink_gate_srtq128n512t2048_kernel(
                 accum_out=neg_max,
             )
 
-        p_sb = sb.tile([P, N + 1], F32, name="p_sb", align_bytes=64)
+        planes = neg[:, 0:N].rearrange("q (e b u j) -> q u e b j", e=2, b=BLOCKS, u=2)
+        p_sb = sb.tile([P, PACK, P], F32, name="p_sb", align_bytes=64)
         p_ps = ps.tile([P, PACK, P], F32, name="p_ps")
         for t in range(PACK):
-            cols = slice(t * P, (t + 1) * P + (t == PACK - 1))
-            nc.scalar.activation(p_sb[:, cols], neg[:, cols], ACT.Exp, bias=neg_max, scale=-1.0)
-            nc.tensor.transpose(p_ps[:, t, :], p_sb[:, t * P : (t + 1) * P], ident[:])
+            nc.scalar.activation(
+                p_sb[:, t, :].rearrange("q (b j) -> q b j", b=BLOCKS),
+                planes[:, t // 2, t % 2, :, :],
+                ACT.Exp,
+                bias=neg_max,
+                scale=-1.0,
+            )
+            nc.tensor.transpose(p_ps[:, t, :], p_sb[:, t, :], ident[:])
 
         v_g = sb.tile([P, N], BF16, name="v_g", align_bytes=64)
         v_words = v_g[:].bitcast(F32)
-        nc.vector.tensor_copy(v_g[:], listed(v_pool[:], 0, N))
+        v_runs = v_g[:].rearrange("e (u b x) -> e b u x", u=2, x=RUN)
+        for h in range(2):
+            nc.vector.tensor_copy(
+                v_runs[:, h * BLOCKS // 2 : (h + 1) * BLOCKS // 2, :, :],
+                listed(v_pool[:, : (PREFIX, T)[h]], h * HALF, (h + 1) * HALF),
+            )
         w_q = reuse.tile([P, NQ, PACK], BF16, name="w_q", offset=0, align_bytes=64)
         for g in range(2):
             queries = slice(g * NQ // 2, (g + 1) * NQ // 2)
@@ -156,12 +175,12 @@ def tile_attend_soft_sink_gate_srtq128n512t2048_kernel(
             )
         summed = sb.tile([P, N + 1], F32, name="summed", align_bytes=64)
         total = sb.tile([P, 1], F32, name="total")
-        nc.scalar.activation(summed[:], p_sb[:], ACT.Identity, accum_out=total[:])
+        nc.scalar.activation(summed[:], neg[:], ACT.Exp, bias=neg_max, scale=-1.0, accum_out=total[:])
         half_tanh = sb.tile([P, DV], F32, name="half_tanh", align_bytes=64)
         nc.scalar.activation(half_tanh[:], gate_in[:], ACT.Tanh, scale=0.5)
         v_ps = ps.tile([P, 2, DV], F32, name="v_ps")
         for u in range(2):
-            nc.tensor.transpose(v_ps[:, u, :], v_words[:, u::2], ident[:])
+            nc.tensor.transpose(v_ps[:, u, :], v_words[:, u * P : (u + 1) * P], ident[:])
         v_q = sb.tile([P, DV, PACK], BF16, name="v_q", align_bytes=64)
         for g in range(2):
             cols = slice(g * DV // 2, (g + 1) * DV // 2)

@@ -51,9 +51,11 @@ def tile_attend_soft_sink_gate_srtq128n512t2048_kernel(
         gate_in = sb.tile([P, DV], F32, name="gate_in")
         sink_col = sb.tile([P, 1], F32, name="sink_col")
         ones = sb.tile([P, P], F32, name="ones", align_bytes=64)
-        ramp = sb.tile([P, P], F32, name="ramp", tag="ramp", align_bytes=64)
+        ramp = sb.tile([P, P], F32, name="ramp", align_bytes=64)
         ramp_t = sb.tile([P, 32], F32, name="ramp_t", align_bytes=64)
         first_lane = sb.tile([P, 1], F32, name="first_lane")
+        neg_lane = sb.tile([P, 1], F32, name="neg_lane")
+        apart = sb.tile([P, P], F32, name="apart", align_bytes=64)
         ident = sb.tile([P, P], F32, name="ident", align_bytes=64)
 
         nc.vector.memset(ks_pool[:].bitcast(I32), 0)
@@ -70,8 +72,8 @@ def tile_attend_soft_sink_gate_srtq128n512t2048_kernel(
         nc.scalar.dma_start(vs_pool[VS_ROW : VS_ROW + 1, :], vs[0:1, :])
         nc.sync.dma_start(kw_pool[:, :K_CUT].bitcast(I32), k_all[:, :K_CUT])
         nc.sync.dma_start(offsets[:], offs)
-        for quad in range(4):
-            nc.sync.dma_start(ks_pool[32 * quad : 32 * quad + 4, :].bitcast(I32), k_rows[4 * quad : 4 * quad + 4, :])
+        for row in range(4):
+            nc.sync.dma_start(ks_pool[row:P:32, :].bitcast(I32), k_rows[row:16:4, :])
         nc.sync.dma_start(kw_pool[:, K_CUT:PREFIX].bitcast(I32), k_all[:, K_CUT:PREFIX])
         nc.sync.dma_start(
             qs[0 : REPEATS * PERIOD, :].bitcast(I32),
@@ -87,8 +89,10 @@ def tile_attend_soft_sink_gate_srtq128n512t2048_kernel(
 
         for quad in range(4):
             rows = slice(32 * quad, 32 * quad + 32)
-            nc.scalar.activation(first_lane[rows, :], ones[rows, 0:1], ACT.Copy, scale=32.0 * quad)
-        nc.vector.tensor_scalar(ident[:], ramp[:], first_lane[:], ramp_t[:, 0:1], ALU.subtract, ALU.is_equal)
+            nc.scalar.activation(first_lane[rows, :], ones[rows, 0:1], ACT.Copy, scale=-32.0 * quad)
+        nc.scalar.activation(neg_lane[:], ramp_t[:, 0:1], ACT.Identity, scale=-1.0, bias=first_lane[:])
+        nc.scalar.activation(apart[:], ramp[:], ACT.Abs, bias=neg_lane[:])
+        nc.scalar.activation(ident[:], apart[:], ACT.Relu, scale=-1.0, bias=ones[:, 0:1])
 
         def listed(pool, first, last):
             return pool.indirect(offsets[:, first // 16 : last // 16])
@@ -100,19 +104,14 @@ def tile_attend_soft_sink_gate_srtq128n512t2048_kernel(
             vs_planes[:].rearrange("p (u e) (b j) -> p u e b j", u=2, b=BLOCKS),
             vs_g[:].rearrange("p (b u j e) -> p u e b j", b=BLOCKS, u=2, e=2),
         )
-        vs_ps = ps.tile([P, PACK, P], F32, name="vs_ps")
-        for t in range(PACK):
-            nc.tensor.transpose(vs_ps[:, t, :], vs_planes[:, t, :], ident[:])
-        vs_col = sb.tile([P, PACK], F32, name="vs_col")
-        nc.scalar.copy(vs_col[:], vs_ps[:, :, VS_ROW])
 
-        ks_g = sb.tile([P, N], U8, name="ks_g", tag="ramp", align_bytes=64)
+        ks_g = sb.tile([P, N], U8, name="ks_g", align_bytes=64)
         nc.vector.tensor_copy(ks_g[:], listed(ks_pool[:], 0, N))
 
         neg = sb.tile([P, N + 1], F32, name="neg", align_bytes=64)
         nc.scalar.mul(neg[:, N : N + 1], sink_col[:], -1.0)
 
-        scores = [ps.tile([P, HALF], F32, name=f"scores{h}") for h in range(2)]
+        scores = [ps.tile([P, HALF], F32, name=f"scores{h}", tag=f"scores{h}") for h in range(2)]
         for h in range(2):
             kw_g = sb.tile([P, HALF], U32, name=f"kw_g{h}", align_bytes=64)
             nc.vector.tensor_copy(kw_g[:], listed(kw_pool[:, : (PREFIX, T)[h]], h * HALF, (h + 1) * HALF))
@@ -143,6 +142,10 @@ def tile_attend_soft_sink_gate_srtq128n512t2048_kernel(
                 accum_out=neg_max,
             )
 
+        vs_ps = ps.tile([P, PACK, P], F32, name="vs_ps", tag="scores0")
+        for t in range(PACK):
+            nc.tensor.transpose(vs_ps[:, t, :], vs_planes[:, t, :], ident[:])
+
         planes = neg[:, 0:N].rearrange("q (e b u j) -> q u e b j", e=2, b=BLOCKS, u=2)
         p_sb = sb.tile([P, PACK, P], F32, name="p_sb", align_bytes=64)
         p_ps = ps.tile([P, PACK, P], F32, name="p_ps")
@@ -155,6 +158,9 @@ def tile_attend_soft_sink_gate_srtq128n512t2048_kernel(
                 scale=-1.0,
             )
             nc.tensor.transpose(p_ps[:, t, :], p_sb[:, t, :], ident[:])
+
+        vs_col = sb.tile([P, PACK], F32, name="vs_col")
+        nc.scalar.copy(vs_col[:], vs_ps[:, :, VS_ROW])
 
         v_g = sb.tile([P, N], BF16, name="v_g", align_bytes=64)
         v_words = v_g[:].bitcast(F32)

@@ -85,7 +85,9 @@ def tile_attend_soft_sink_gate_srtq128n512t2048_kernel(
         nc.sync.dma_start(sink_col[:], sink[0])
         nc.sync.dma_start(v_pool[:, :PREFIX], vT[:, :PREFIX])
         nc.sync.dma_start(v_pool[:, PREFIX:], vT[:, PREFIX:])
-        nc.sync.dma_start(gate_in[:], og[0])
+        for part in range(8):
+            rows = slice(16 * part, 16 * part + 16)
+            nc.sync.dma_start(gate_in[rows, :], og[0][rows, :])
 
         for quad in range(4):
             rows = slice(32 * quad, 32 * quad + 32)
@@ -193,7 +195,7 @@ def tile_attend_soft_sink_gate_srtq128n512t2048_kernel(
             nc.scalar.copy(v_q[:, cols, :].bitcast(F32), v_ps[:, :, cols].rearrange("s u e -> s e u"))
 
         gate = sb.tile([P, DV], F32, name="gate")
-        nc.scalar.activation(gate[:], half_tanh[:], ACT.Copy, bias=0.5, scale=0.5)
+        nc.vector.tensor_scalar(gate[:], half_tanh[:], 0.5, 0.5, ALU.mult, ALU.add)
 
         w_codes = sb.tile([P, NQ], U32, name="w_codes", align_bytes=64)
         w_scales = sb.tile([P, NQ], U8, name="w_scales", align_bytes=64)

@@ -54,15 +54,15 @@ def tile_attend_soft_sink_gate_srtq128n512t2048_kernel(
         ramp = sb.tile([P, P], F32, name="ramp", align_bytes=64)
         ramp_t = sb.tile([P, 32], F32, name="ramp_t", align_bytes=64)
         first_lane = sb.tile([P, 1], F32, name="first_lane")
-        neg_lane = sb.tile([P, 1], F32, name="neg_lane")
-        apart = sb.tile([P, P], F32, name="apart", align_bytes=64)
         ident = sb.tile([P, P], F32, name="ident", align_bytes=64)
 
         nc.vector.memset(ks_pool[:].bitcast(I32), 0)
         nc.vector.memset(ones[:], 1.0)
         nc.vector.memset(qs[:].bitcast(I32), 0)
-        nc.vector.tensor_tensor_scan(ramp[:], ones[:], ones[:], 0.0, ALU.mult, ALU.add)
         nc.vector.memset(vs_pool[0:VS_ROW, :].bitcast(I32), 0)
+        nc.vector.tensor_tensor_scan(ramp[:], ones[:], ones[:], 0.0, ALU.mult, ALU.add)
+        for quad in range(3):
+            nc.vector.memset(first_lane[32 * quad : 32 * quad + 32, :], 32.0 * quad)
         nc.vector.transpose(ramp_t[:], ramp[:, :32])
 
         q_rows = q_scales[0, 0].bitcast(I32)
@@ -89,12 +89,8 @@ def tile_attend_soft_sink_gate_srtq128n512t2048_kernel(
             rows = slice(16 * part, 16 * part + 16)
             nc.sync.dma_start(gate_in[rows, :], og[0][rows, :])
 
-        for quad in range(4):
-            rows = slice(32 * quad, 32 * quad + 32)
-            nc.scalar.activation(first_lane[rows, :], ones[rows, 0:1], ACT.Copy, scale=-32.0 * quad)
-        nc.scalar.activation(neg_lane[:], ramp_t[:, 0:1], ACT.Identity, scale=-1.0, bias=first_lane[:])
-        nc.scalar.activation(apart[:], ramp[:], ACT.Abs, bias=neg_lane[:])
-        nc.scalar.activation(ident[:], apart[:], ACT.Relu, scale=-1.0, bias=ones[:, 0:1])
+        nc.scalar.activation(first_lane[96:P, :], ones[96:P, 0:1], ACT.Copy, scale=96.0)
+        nc.vector.tensor_scalar(ident[:], ramp[:], first_lane[:], ramp_t[:, 0:1], ALU.subtract, ALU.is_equal)
 
         def listed(pool, first, last):
             return pool.indirect(offsets[:, first // 16 : last // 16])

@@ -17,6 +17,9 @@ PERIOD = 14
 REPEATS = 5
 BLOCKS = N // 32
 RUN = 16
+FIRST = 224
+K_PREFIX = T - N + FIRST
+EARLY = 192
 
 FLOPS = 2 * NQ * N * D + 2 * NQ * N * DV
 BYTES = P * T * 4 + 16 * T + P * NQ * 4 + 16 * NQ + DV * T * 4 + T * 4 + NQ * 4 + 2 * NQ * DV * 4 + P * (N // 16) * 2
@@ -74,12 +77,12 @@ def tile_attend_soft_sink_gate_srtq128n512t2048_kernel(
         nc.sync.dma_start(offsets[:], offs)
         for row in range(4):
             nc.sync.dma_start(ks_pool[row:P:32, :].bitcast(I32), k_rows[row:16:4, :])
-        nc.sync.dma_start(kw_pool[:, K_CUT:PREFIX].bitcast(I32), k_all[:, K_CUT:PREFIX])
+        nc.sync.dma_start(kw_pool[:, K_CUT:K_PREFIX].bitcast(I32), k_all[:, K_CUT:K_PREFIX])
         nc.sync.dma_start(
             qs[0 : REPEATS * PERIOD, :].bitcast(I32),
             q_rows[0:PERIOD, :].unsqueeze(0).broadcast_to([REPEATS, PERIOD, NQ // 4]),
         )
-        nc.sync.dma_start(kw_pool[:, PREFIX:].bitcast(I32), k_all[:, PREFIX:])
+        nc.sync.dma_start(kw_pool[:, K_PREFIX:].bitcast(I32), k_all[:, K_PREFIX:])
         nc.sync.dma_start(qw[:].bitcast(I32), q_words[0, 0].rearrange("p n t -> p (n t)").bitcast(I32))
         nc.sync.dma_start(qs[96:100, :].bitcast(I32), q_rows[12:16, :])
         nc.sync.dma_start(sink_col[:], sink[0])
@@ -109,16 +112,18 @@ def tile_attend_soft_sink_gate_srtq128n512t2048_kernel(
         neg = sb.tile([P, N + 1], F32, name="neg", align_bytes=64)
         nc.scalar.mul(neg[:, N : N + 1], sink_col[:], -1.0)
 
-        scores = [ps.tile([P, HALF], F32, name=f"scores{h}", tag=f"scores{h}") for h in range(2)]
-        for h in range(2):
-            kw_g = sb.tile([P, HALF], U32, name=f"kw_g{h}", align_bytes=64)
-            nc.vector.tensor_copy(kw_g[:], listed(kw_pool[:, : (PREFIX, T)[h]], h * HALF, (h + 1) * HALF))
+        scores = [ps.tile([P, (EARLY, N - EARLY)[h]], F32, name=f"scores{h}", tag=f"scores{h}") for h in range(2)]
+        kw_g = sb.tile([P, N], U32, name="kw_g", align_bytes=64)
+        for first, last, window in ((0, FIRST, K_PREFIX), (FIRST, 3 * P, T), (3 * P, N, T)):
+            nc.vector.tensor_copy(kw_g[:, first:last], listed(kw_pool[:, :window], first, last))
+        for first, last in ((0, P), (P, EARLY), (EARLY, 2 * P), (2 * P, 3 * P), (3 * P, N)):
+            bank = 0 if first < EARLY else 1
             nc.tensor.matmul_mx(
-                out=scores[h][:],
+                out=scores[bank][:, first - bank * EARLY : last - bank * EARLY],
                 lhsT=qw[:].bitcast(FP8X4),
                 lhsT_scale=qs[:],
-                rhs=kw_g[:].bitcast(FP8X4),
-                rhs_scale=ks_g[:, h * HALF : (h + 1) * HALF],
+                rhs=kw_g[:, first:last].bitcast(FP8X4),
+                rhs_scale=ks_g[:, first:last],
                 start=True,
                 stop=True,
             )
@@ -131,7 +136,7 @@ def tile_attend_soft_sink_gate_srtq128n512t2048_kernel(
             so_far = neg_max
             neg_max = (half_max[:], row_max[:])[h]
             nc.vector.tensor_scalar(
-                by_parity[:, :, h * P : (h + 1) * P],
+                by_parity[:, :, (0, EARLY // 2)[h] : (EARLY // 2, N // 2)[h]],
                 scores[h][:].rearrange("q (w e) -> q e w", e=2),
                 -1.0,
                 so_far,

@@ -52,7 +52,7 @@ def tile_attend_soft_sink_gate_srtq128n512t2048_kernel(
         qw = sb.tile([P, NQ], U32, name="qw", align_bytes=64)
         qs = sb.tile([P, NQ], U8, name="qs", align_bytes=64)
         gate_in = sb.tile([P, DV], F32, name="gate_in")
-        sink_col = sb.tile([P, 1], F32, name="sink_col")
+        sink_rows = sb.tile([P, 32], F32, name="sink_rows", align_bytes=64)
         ones = sb.tile([P, P], F32, name="ones", align_bytes=64)
         ramp = sb.tile([P, P], F32, name="ramp", align_bytes=64)
         ramp_t = sb.tile([P, 32], F32, name="ramp_t", align_bytes=64)
@@ -63,6 +63,7 @@ def tile_attend_soft_sink_gate_srtq128n512t2048_kernel(
         nc.vector.memset(ones[:], 1.0)
         nc.vector.memset(qs[:].bitcast(I32), 0)
         nc.vector.memset(vs_pool[0:VS_ROW, :].bitcast(I32), 0)
+        nc.vector.memset(sink_rows[:], 0.0)
         nc.vector.tensor_tensor_scan(ramp[:], ones[:], ones[:], 0.0, ALU.mult, ALU.add)
         for quad in range(3):
             nc.vector.memset(first_lane[32 * quad : 32 * quad + 32, :], 32.0 * quad)
@@ -85,7 +86,7 @@ def tile_attend_soft_sink_gate_srtq128n512t2048_kernel(
         nc.sync.dma_start(kw_pool[:, K_PREFIX:].bitcast(I32), k_all[:, K_PREFIX:])
         nc.sync.dma_start(qw[:].bitcast(I32), q_words[0, 0].rearrange("p n t -> p (n t)").bitcast(I32))
         nc.sync.dma_start(qs[96:100, :].bitcast(I32), q_rows[12:16, :])
-        nc.sync.dma_start(sink_col[:], sink[0])
+        nc.sync.dma_start(sink_rows[0:P:32, :], sink[0].rearrange("(quad q) one -> quad (q one)", quad=4))
         nc.sync.dma_start(v_pool[:, :PREFIX], vT[:, :PREFIX])
         nc.sync.dma_start(v_pool[:, PREFIX:], vT[:, PREFIX:])
         for part in range(8):
@@ -109,8 +110,10 @@ def tile_attend_soft_sink_gate_srtq128n512t2048_kernel(
         ks_g = sb.tile([P, N], U8, name="ks_g", align_bytes=64)
         nc.vector.tensor_copy(ks_g[:], listed(ks_pool[:], 0, N))
 
-        neg = sb.tile([P, N + 1], F32, name="neg", align_bytes=64)
-        nc.scalar.mul(neg[:, N : N + 1], sink_col[:], -1.0)
+        neg = sb.tile([P, N + 32], F32, name="neg", align_bytes=64)
+        neg_rows = sb.tile([P, 32], F32, name="neg_rows", align_bytes=64)
+        nc.scalar.mul(neg_rows[:], sink_rows[:], -1.0)
+        nc.vector.transpose(neg[:, N:], neg_rows[:])
 
         scores = [ps.tile([P, (EARLY, N - EARLY)[h]], F32, name=f"scores{h}", tag=f"scores{h}") for h in range(2)]
         kw_g = sb.tile([P, N], U32, name="kw_g", align_bytes=64)
@@ -184,7 +187,7 @@ def tile_attend_soft_sink_gate_srtq128n512t2048_kernel(
             )
         summed = sb.tile([P, N + 1], F32, name="summed", align_bytes=64)
         total = sb.tile([P, 1], F32, name="total")
-        nc.scalar.activation(summed[:], neg[:], ACT.Exp, bias=neg_max, scale=-1.0, accum_out=total[:])
+        nc.scalar.activation(summed[:], neg[:, : N + 1], ACT.Exp, bias=neg_max, scale=-1.0, accum_out=total[:])
         half_tanh = sb.tile([P, DV], F32, name="half_tanh", align_bytes=64)
         nc.scalar.activation(half_tanh[:], gate_in[:], ACT.Tanh, scale=0.5)
         v_ps = ps.tile([P, 2, DV], F32, name="v_ps")

from contextlib import ExitStack

import concourse.mybir as mybir

P = 128
T = 2048
N = 512
NQ = 128
DV = 128
D = 512
PACK = 4
HALF = N // 2
VS_ROW = P - 1
K_CUT = 448
PREFIX = T - HALF
PERIOD = 14
REPEATS = 5
BLOCKS = N // 32
RUN = 16
FIRST = 224
K_PREFIX = T - N + FIRST
EARLY = 192

FLOPS = 2 * NQ * N * D + 2 * NQ * N * DV
BYTES = P * T * 4 + 16 * T + P * NQ * 4 + 16 * NQ + DV * T * 4 + T * 4 + NQ * 4 + 2 * NQ * DV * 4 + P * (N // 16) * 2

F32 = mybir.dt.float32
BF16 = mybir.dt.bfloat16
I32 = mybir.dt.int32
U32 = mybir.dt.uint32
U16 = mybir.dt.uint16
U8 = mybir.dt.uint8
FP8X4 = mybir.dt.float8_e4m3fn_x4
ALU = mybir.AluOpType
ACT = mybir.ActivationFunctionType


def tile_attend_soft_sink_gate_srtq128n512t2048_kernel(
    tc, q_words, q_scales, k_words, k_scales, vT, vs, sink, og, offs, out
):
    nc = tc.nc
    with ExitStack() as ctx:
        sb = ctx.enter_context(tc.tile_pool(name="sb", bufs=1))
        reuse = ctx.enter_context(tc.tile_pool(name="reuse", bufs=1))
        ps = ctx.enter_context(tc.psum_pool(name="ps", bufs=1))

        offsets = sb.tile([P, N // 16], U16, name="offsets")
        kw_pool = sb.tile([P, T], U32, name="kw_pool", align_bytes=64)
        ks_pool = sb.tile([P, T], U8, name="ks_pool", align_bytes=64)
        v_pool = reuse.tile([P, T], F32, name="v_pool", offset=0, align_bytes=64)
        vs_pool = sb.tile([P, T], F32, name="vs_pool", align_bytes=64)
        qw = sb.tile([P, NQ], U32, name="qw", align_bytes=64)
        qs = sb.tile([P, NQ], U8, name="qs", align_bytes=64)
        gate_in = sb.tile([P, DV], F32, name="gate_in")
        sink_rows = sb.tile([P, 32], F32, name="sink_rows", align_bytes=64)
        ones = sb.tile([P, P], F32, name="ones", align_bytes=64)
        ramp = sb.tile([P, P], F32, name="ramp", align_bytes=64)
        ramp_t = sb.tile([P, 32], F32, name="ramp_t", align_bytes=64)
        first_lane = sb.tile([P, 1], F32, name="first_lane")
        ident = sb.tile([P, P], F32, name="ident", align_bytes=64)

        nc.vector.memset(ks_pool[:].bitcast(I32), 0)
        nc.vector.memset(ones[:], 1.0)
        nc.vector.memset(qs[:].bitcast(I32), 0)
        nc.vector.memset(vs_pool[0:VS_ROW, :].bitcast(I32), 0)
        nc.vector.memset(sink_rows[:], 0.0)
        nc.vector.tensor_tensor_scan(ramp[:], ones[:], ones[:], 0.0, ALU.mult, ALU.add)
        for quad in range(3):
            nc.vector.memset(first_lane[32 * quad : 32 * quad + 32, :], 32.0 * quad)
        nc.vector.transpose(ramp_t[:], ramp[:, :32])

        q_rows = q_scales[0, 0].bitcast(I32)
        k_rows = k_scales[0].bitcast(I32)
        k_all = k_words[0].rearrange("p n t -> p (n t)").bitcast(I32)

        nc.scalar.dma_start(vs_pool[VS_ROW : VS_ROW + 1, :], vs[0:1, :])
        nc.sync.dma_start(kw_pool[:, :K_CUT].bitcast(I32), k_all[:, :K_CUT])
        nc.sync.dma_start(offsets[:], offs)
        for row in range(4):
            nc.sync.dma_start(ks_pool[row:P:32, :].bitcast(I32), k_rows[row:16:4, :])
        nc.sync.dma_start(kw_pool[:, K_CUT:K_PREFIX].bitcast(I32), k_all[:, K_CUT:K_PREFIX])
        nc.sync.dma_start(
            qs[0 : REPEATS * PERIOD, :].bitcast(I32),
            q_rows[0:PERIOD, :].unsqueeze(0).broadcast_to([REPEATS, PERIOD, NQ // 4]),
        )
        nc.sync.dma_start(kw_pool[:, K_PREFIX:].bitcast(I32), k_all[:, K_PREFIX:])
        nc.sync.dma_start(qw[:].bitcast(I32), q_words[0, 0].rearrange("p n t -> p (n t)").bitcast(I32))
        nc.sync.dma_start(qs[96:100, :].bitcast(I32), q_rows[12:16, :])
        nc.sync.dma_start(sink_rows[0:P:32, :], sink[0].rearrange("(quad q) one -> quad (q one)", quad=4))
        nc.sync.dma_start(v_pool[:, :PREFIX], vT[:, :PREFIX])
        nc.sync.dma_start(v_pool[:, PREFIX:], vT[:, PREFIX:])
        for part in range(8):
            rows = slice(16 * part, 16 * part + 16)
            nc.sync.dma_start(gate_in[rows, :], og[0][rows, :])

        nc.scalar.activation(first_lane[96:P, :], ones[96:P, 0:1], ACT.Copy, scale=96.0)
        nc.vector.tensor_scalar(ident[:], ramp[:], first_lane[:], ramp_t[:, 0:1], ALU.subtract, ALU.is_equal)

        def listed(pool, first, last):
            return pool.indirect(offsets[:, first // 16 : last // 16])

        vs_g = sb.tile([P, N], F32, name="vs_g", align_bytes=64)
        nc.scalar.activation(vs_g[:], listed(vs_pool[:], 0, N), ACT.Copy)
        vs_planes = sb.tile([P, PACK, P], F32, name="vs_planes", align_bytes=64)
        nc.scalar.copy(
            vs_planes[:].rearrange("p (u e) (b j) -> p u e b j", u=2, b=BLOCKS),
            vs_g[:].rearrange("p (b u j e) -> p u e b j", b=BLOCKS, u=2, e=2),
        )

        ks_g = sb.tile([P, N], U8, name="ks_g", align_bytes=64)
        nc.vector.tensor_copy(ks_g[:], listed(ks_pool[:], 0, N))

        neg = sb.tile([P, N + 32], F32, name="neg", align_bytes=64)
        neg_rows = sb.tile([P, 32], F32, name="neg_rows", align_bytes=64)
        nc.scalar.mul(neg_rows[:], sink_rows[:], -1.0)
        nc.vector.transpose(neg[:, N:], neg_rows[:])

        scores = [ps.tile([P, (EARLY, N - EARLY)[h]], F32, name=f"scores{h}", tag=f"scores{h}") for h in range(2)]
        kw_g = sb.tile([P, N], U32, name="kw_g", align_bytes=64)
        for first, last, window in ((0, FIRST, K_PREFIX), (FIRST, 3 * P, T), (3 * P, N, T)):
            nc.vector.tensor_copy(kw_g[:, first:last], listed(kw_pool[:, :window], first, last))
        for first, last in ((0, P), (P, EARLY), (EARLY, 2 * P), (2 * P, 3 * P), (3 * P, N)):
            bank = 0 if first < EARLY else 1
            nc.tensor.matmul_mx(
                out=scores[bank][:, first - bank * EARLY : last - bank * EARLY],
                lhsT=qw[:].bitcast(FP8X4),
                lhsT_scale=qs[:],
                rhs=kw_g[:, first:last].bitcast(FP8X4),
                rhs_scale=ks_g[:, first:last],
                start=True,
                stop=True,
            )

        by_parity = neg[:, 0:N].rearrange("q (e w) -> q e w", e=2)
        half_max = sb.tile([P, 1], F32, name="half_max")
        row_max = sb.tile([P, 1], F32, name="row_max")
        neg_max = neg[:, N : N + 1]
        for h in range(2):
            so_far = neg_max
            neg_max = (half_max[:], row_max[:])[h]
            nc.vector.tensor_scalar(
                by_parity[:, :, (0, EARLY // 2)[h] : (EARLY // 2, N // 2)[h]],
                scores[h][:].rearrange("q (w e) -> q e w", e=2),
                -1.0,
                so_far,
                ALU.mult,
                ALU.min,
                accum_out=neg_max,
            )

        vs_ps = ps.tile([P, PACK, P], F32, name="vs_ps", tag="scores0")
        for t in range(PACK):
            nc.tensor.transpose(vs_ps[:, t, :], vs_planes[:, t, :], ident[:])

        planes = neg[:, 0:N].rearrange("q (e b u j) -> q u e b j", e=2, b=BLOCKS, u=2)
        p_sb = sb.tile([P, PACK, P], F32, name="p_sb", align_bytes=64)
        p_ps = ps.tile([P, PACK, P], F32, name="p_ps")
        for t in range(PACK):
            nc.scalar.activation(
                p_sb[:, t, :].rearrange("q (b j) -> q b j", b=BLOCKS),
                planes[:, t // 2, t % 2, :, :],
                ACT.Exp,
                bias=neg_max,
                scale=-1.0,
            )
            nc.tensor.transpose(p_ps[:, t, :], p_sb[:, t, :], ident[:])

        vs_col = sb.tile([P, PACK], F32, name="vs_col")
        nc.scalar.copy(vs_col[:], vs_ps[:, :, VS_ROW])

        v_g = sb.tile([P, N], BF16, name="v_g", align_bytes=64)
        v_words = v_g[:].bitcast(F32)
        v_runs = v_g[:].rearrange("e (u b x) -> e b u x", u=2, x=RUN)
        for h in range(2):
            nc.vector.tensor_copy(
                v_runs[:, h * BLOCKS // 2 : (h + 1) * BLOCKS // 2, :, :],
                listed(v_pool[:, : (PREFIX, T)[h]], h * HALF, (h + 1) * HALF),
            )
        w_q = reuse.tile([P, NQ, PACK], BF16, name="w_q", offset=0, align_bytes=64)
        for g in range(2):
            queries = slice(g * NQ // 2, (g + 1) * NQ // 2)
            nc.vector.tensor_tensor(
                w_q[:, queries, :],
                p_ps[:, :, queries].rearrange("s t q -> s q t"),
                vs_col[:].unsqueeze(1).broadcast_to([P, NQ // 2, PACK]),
                ALU.mult,
            )
        summed = sb.tile([P, N + 1], F32, name="summed", align_bytes=64)
        total = sb.tile([P, 1], F32, name="total")
        nc.scalar.activation(summed[:], neg[:, : N + 1], ACT.Exp, bias=neg_max, scale=-1.0, accum_out=total[:])
        half_tanh = sb.tile([P, DV], F32, name="half_tanh", align_bytes=64)
        nc.scalar.activation(half_tanh[:], gate_in[:], ACT.Tanh, scale=0.5)
        v_ps = ps.tile([P, 2, DV], F32, name="v_ps")
        for u in range(2):
            nc.tensor.transpose(v_ps[:, u, :], v_words[:, u * P : (u + 1) * P], ident[:])
        v_q = sb.tile([P, DV, PACK], BF16, name="v_q", align_bytes=64)
        for g in range(2):
            cols = slice(g * DV // 2, (g + 1) * DV // 2)
            nc.scalar.copy(v_q[:, cols, :].bitcast(F32), v_ps[:, :, cols].rearrange("s u e -> s e u"))

        gate = sb.tile([P, DV], F32, name="gate")
        nc.vector.tensor_scalar(gate[:], half_tanh[:], 0.5, 0.5, ALU.mult, ALU.add)

        w_codes = sb.tile([P, NQ], U32, name="w_codes", align_bytes=64)
        w_scales = sb.tile([P, NQ], U8, name="w_scales", align_bytes=64)
        v_codes = sb.tile([P, DV], U32, name="v_codes", align_bytes=64)
        v_scales = sb.tile([P, DV], U8, name="v_scales", align_bytes=64)
        y = sb.tile([P, DV], F32, name="y")
        y_ps = [ps.tile([P, DV // 2], F32, name=f"y_ps{g}") for g in range(2)]

        def quantise_values(g):
            cols = slice(g * DV // 2, (g + 1) * DV // 2)
            nc.vector.quantize_mx(
                out=v_codes[:, cols].bitcast(FP8X4),
                scales=v_scales[:, cols],
                in_=v_q[:, cols, :].rearrange("s e t -> s (e t)"),
            )

        for g in range(2):
            queries = slice(g * NQ // 2, (g + 1) * NQ // 2)
            nc.vector.quantize_mx(
                out=w_codes[:, queries].bitcast(FP8X4),
                scales=w_scales[:, queries],
                in_=w_q[:, queries, :].rearrange("s q t -> s (q t)"),
            )
        quantise_values(0)
        quantise_values(1)
        inv_total = reuse.tile([P, 1], F32, name="inv_total", offset=2 * N, align_bytes=64)
        nc.vector.reciprocal(inv_total[:], total[:])
        for g in range(2):
            cols = slice(g * DV // 2, (g + 1) * DV // 2)
            nc.tensor.matmul_mx(
                out=y_ps[g][:],
                lhsT=w_codes[:].bitcast(FP8X4),
                lhsT_scale=w_scales[:],
                rhs=v_codes[:, cols].bitcast(FP8X4),
                rhs_scale=v_scales[:, cols],
                start=True,
                stop=True,
            )
        for g in range(2):
            cols = slice(g * DV // 2, (g + 1) * DV // 2)
            nc.vector.scalar_tensor_tensor(y[:, cols], y_ps[g][:], inv_total[:], gate[:, cols], ALU.mult, ALU.mult)
        nc.sync.dma_start(out[0], y[:])
